import numpy as np
import ml_dtypes


def mxq(x, axis, fmt="e4m3"):
    dtype, down = {"e4m3": (ml_dtypes.float8_e4m3fn, 7), "e5m2": (ml_dtypes.float8_e5m2, 14)}[fmt]
    v = np.moveaxis(np.asarray(x, np.float32).astype(ml_dtypes.bfloat16).astype(np.float64), axis, -1)
    blocks = v.reshape(v.shape[:-1] + (-1, 32))
    amax = np.abs(blocks).max(-1, keepdims=True)
    byte = np.maximum(np.where(amax > 0, np.frexp(amax)[1] - 1 + 127, 0) - down, 1)
    scale = np.exp2(byte - 127.0)
    codes = (blocks / scale).astype(np.float32).astype(dtype).astype(np.float64)
    return np.moveaxis((codes * scale).reshape(v.shape), -1, axis)


WIDE = False


def mx_kscale(k):
    if not WIDE:
        return np.ones(k)
    levels = np.array([10, -10, 5, -5, 0])
    if k % 512:
        return np.exp2(np.random.permutation(np.resize(levels, k // 32))).repeat(32)
    a = np.empty((k // 512, 16))
    for p in range(k // 512):
        a[p, :8] = np.random.permutation(np.resize(levels, 8))
        for g in range(8):
            far = levels[np.abs(levels - a[p, g]) >= 10]
            a[p, g + 8] = far[np.random.randint(len(far))]
    return np.exp2(a.ravel()).repeat(32)


def f64(x):
    return np.asarray(x).astype(np.float64)


def striped(idx):
    return np.tile(idx.reshape(-1, 16).T, (8, 1)).astype(np.uint16)


def unstriped(offs):
    return offs[:16].T.reshape(-1).astype(np.int64)


def pack_weight(w):
    k, n = w.shape
    w = f64(np.asarray(w, np.float32).astype(ml_dtypes.bfloat16)).reshape(k // 32, 32, n)
    amax = np.abs(w).max(1)
    byte = np.clip(np.where(amax > 0, np.frexp(amax)[1] - 1 + 127 - 7, 1), 1, 254)
    scaled = (w * np.exp2(127.0 - byte)[:, None, :]).reshape(k, n).astype(np.float32)
    words = np.ascontiguousarray(scaled.reshape(k // 512, 128, 4, n).transpose(0, 1, 3, 2)).astype(ml_dtypes.float8_e4m3fn).view(np.uint8)
    return words, np.ascontiguousarray(byte.astype(np.uint8).reshape(k // 512, 16, n))


def unpack_weight(words, scales):
    g, p, n, _ = words.shape
    vals = np.ascontiguousarray(words).view(ml_dtypes.float8_e4m3fn).astype(np.float64) * np.repeat(np.exp2(scales.astype(np.float64) - 127.0), 8, axis=1)[..., None]
    return vals.transpose(0, 1, 3, 2).reshape(g * 512, n)


K, T, N, U = 1024, 1024, 128, 2048
P = 2 ** 7


def setup_inputs():
    n = np.random.standard_normal
    s = mx_kscale(K)[:, None]
    packed_xT = pack_weight(n((K, T)) * s)
    return {
        "x_words": packed_xT[0],
        "x_scales": packed_xT[1],
        "mem": n((N, U)).astype(np.float32),
        "w1": (n((K, N)) / np.sqrt(K) / s).astype(np.float32),
        "old": np.tile(np.random.uniform(0.5, 0.95, T), (P, 1)).astype(np.float32),
        "new": np.tile(np.random.uniform(0.05, 0.5, T), (P, 1)).astype(np.float32),
        "slot": striped(np.random.permutation(U)[:T]),
    }


def reference(x_words, x_scales, mem, w1, old, new, slot):
    xq = unpack_weight(x_words, x_scales)
    y = np.tanh(mxq(f64(w1), 0, "e4m3").T @ xq)
    out = f64(mem).copy()
    out[:, unstriped(slot)] = f64(mem)[:, unstriped(slot)] * f64(old)[:1] + y * f64(new)[:1]
    return out

@@ -1,0 +1,138 @@
+from contextlib import ExitStack
+
+import concourse.mybir as mybir
+from concourse.masks import make_identity
+
+K, T, N, U = 1024, 1024, 128, 2048
+FLOPS = 2 * K * T * N
+BYTES = K * T + K * T // 32 + 4 * (K * N + 2 * N * U + 2 * T) + 2 * 128 * (T // 16)
+
+F32 = mybir.dt.float32
+BF16 = mybir.dt.bfloat16
+I32 = mybir.dt.int32
+U32 = mybir.dt.uint32
+U16 = mybir.dt.uint16
+U8 = mybir.dt.uint8
+FP8X4 = mybir.dt.float8_e4m3fn_x4
+ACT = mybir.ActivationFunctionType
+ALU = mybir.AluOpType
+
+P = 128
+PASSES = K // 512
+BLOCKS = T // P
+CHUNKS = (128, 256, 256, 384)
+
+
+def tile_picked_wema_tanh_l_kernel(tc, x_words, x_scales, mem, w1, old, new, slot, out):
+    nc = tc.nc
+    with ExitStack() as ctx:
+        keep = ctx.enter_context(tc.tile_pool(name="keep", bufs=1))
+        psum = ctx.enter_context(tc.psum_pool(name="psum", bufs=1))
+
+        x_plane = keep.tile([P, T], U8, align_bytes=64)
+        nc.vector.memset(x_plane[:].bitcast(I32), 0)
+        new_rows = keep.tile([P, P], F32)
+        nc.vector.memset(new_rows[:], 0.0)
+        warm_in = keep.tile([P, 1], F32)
+        nc.vector.memset(warm_in[:], 0.0)
+        warm_out = keep.tile([P, 1], F32)
+        nc.scalar.activation(out=warm_out[:], in_=warm_in[:], func=ACT.Tanh)
+        ident = keep.tile([P, P], F32)
+        make_identity(nc, ident[:])
+
+        old_cols = keep.tile([P, BLOCKS], F32)
+        nc.sync.dma_start(out=old_cols[:], in_=old[0:1, :].rearrange("o (n i) -> (o n) i", i=BLOCKS))
+        w_raw = keep.tile([P, PASSES, 4, N], F32)
+        nc.sync.dma_start(out=w_raw[:], in_=w1.rearrange("(g p j) m -> p g j m", g=PASSES, j=4))
+        offs = keep.tile([P, T // 16], U16)
+        nc.sync.dma_start(out=offs[:], in_=slot)
+        window = keep.tile([P, U], F32)
+        nc.sync.dma_start(out=window[:], in_=mem)
+        nc.sync.dma_start(out=new_rows[0:BLOCKS, :], in_=new[0:1, :].rearrange("o (b c) -> (o b) c", c=P))
+        for q in range(4):
+            nc.sync.dma_start(
+                out=x_plane[32 * q : 32 * q + 4 * PASSES, :].bitcast(I32),
+                in_=x_scales[:, 4 * q : 4 * q + 4, :].bitcast(I32),
+            )
+        x_tiles = []
+        c0 = 0
+        for ci, n in enumerate(CHUNKS):
+            xt = keep.tile([P, PASSES, n], U32, align_bytes=64, name=f"x{ci}")
+            nc.sync.dma_start(
+                out=xt[:].bitcast(I32),
+                in_=x_words[:, :, c0 : c0 + n, :].rearrange("g p n t -> p g (n t)").bitcast(I32),
+            )
+            x_tiles.append(xt)
+            c0 = c0 + n
+
+        w_grouped = keep.tile([P, PASSES, N, 4], BF16, align_bytes=64)
+        nc.vector.tensor_copy(out=w_grouped[:], in_=w_raw[:].rearrange("p g j m -> p g m j"))
+        w_codes = keep.tile([P, PASSES * N], U32, align_bytes=64)
+        w_plane = keep.tile([P, PASSES * N], U8, align_bytes=64)
+        nc.vector.quantize_mx(
+            out=w_codes[:].bitcast(FP8X4),
+            scales=w_plane[:],
+            in_=w_grouped[:].rearrange("p g m j -> p (g m j)"),
+        )
+
+        old_all = keep.tile([P, P, BLOCKS], F32)
+        for h in range(2):
+            spread = psum.tile([P, 4, P], F32, name=f"spread{h}")
+            for i in range(4):
+                col = 4 * h + i
+                nc.tensor.transpose(spread[:, i, :], old_cols[:, col : col + 1].to_broadcast([P, P]), ident[:])
+            nc.scalar.copy(out=old_all[:, :, 4 * h : 4 * h + 4], in_=spread[:].rearrange("p i n -> p n i"))
+
+        new_ps = psum.tile([P, P], F32)
+        nc.tensor.transpose(new_ps[:], new_rows[:], ident[:])
+        new_cols = keep.tile([P, BLOCKS], F32)
+        nc.scalar.copy(out=new_cols[:], in_=new_ps[:, 0:BLOCKS])
+
+        kept = keep.tile([P, T], F32)
+        nc.vector.tensor_tensor(
+            out=kept[:],
+            in0=window[:].indirect(offs[:]),
+            in1=old_all[:].rearrange("p n i -> p (n i)"),
+            op=ALU.mult,
+        )
+
+        c0 = 0
+        for ci, n in enumerate(CHUNKS):
+            xt = x_tiles[ci]
+            nb = n // P
+            acc = psum.tile([P, 512], F32, tag="acc", bufs=3, name=f"acc{ci}")
+            for b in range(nb):
+                for g in range(PASSES):
+                    nc.tensor.matmul_mx(
+                        out=acc[:, b * P : (b + 1) * P],
+                        lhsT=xt[:, g, b * P : (b + 1) * P].bitcast(FP8X4),
+                        lhsT_scale=x_plane[4 * g : P, c0 + b * P : c0 + (b + 1) * P],
+                        rhs=w_codes[:, g * N : (g + 1) * N].bitcast(FP8X4),
+                        rhs_scale=w_plane[:, g * N : (g + 1) * N],
+                        start=(g == 0),
+                        stop=(g == PASSES - 1),
+                    )
+            y_t = keep.tile([P, n], F32, name=f"y{ci}")
+            nc.scalar.activation(out=y_t[:], in_=acc[:, 0:n], func=ACT.Tanh)
+            z_t = keep.tile([P, n], F32, name=f"z{ci}")
+            back = psum.tile([P, 512], F32, tag="back", bufs=2, name=f"back{ci}")
+            for b in range(nb):
+                blk = c0 // P + b
+                nc.scalar.activation(
+                    out=z_t[:, b * P : (b + 1) * P],
+                    in_=y_t[:, b * P : (b + 1) * P],
+                    func=ACT.Copy,
+                    scale=new_cols[:, blk : blk + 1],
+                )
+                nc.tensor.transpose(back[:, b * P : (b + 1) * P], z_t[:, b * P : (b + 1) * P], ident[:])
+            fresh = keep.tile([P, n], F32, name=f"fresh{ci}")
+            nc.scalar.copy(out=fresh[:], in_=back[:, 0:n])
+            nc.vector.tensor_tensor(
+                out=window[:].indirect(offs[:, c0 // 16 : (c0 + n) // 16]),
+                in0=kept[:, c0 : c0 + n],
+                in1=fresh[:],
+                op=ALU.add,
+            )
+            c0 = c0 + n
+
+        nc.sync.dma_start(out=out, in_=window[:])

@@ -1,7 +1,6 @@
 from contextlib import ExitStack
 
 import concourse.mybir as mybir
-from concourse.masks import make_identity
 
 K, T, N, U = 1024, 1024, 128, 2048
 FLOPS = 2 * K * T * N
@@ -18,52 +17,76 @@ ACT = mybir.ActivationFunctionType
 ALU = mybir.AluOpType
 
 P = 128
+BANK = 512
 PASSES = K // 512
 BLOCKS = T // P
-CHUNKS = (128, 256, 256, 384)
+HEAD_GROUPS = (256, 128)
+TAIL_GROUPS = (256, 256, 128)
+LOADS = (256, 128, 256, 384)
+HEAD = sum(HEAD_GROUPS)
+SCATTERS = (384, 640)
+
+
+def spans(widths, start=0):
+    return [(start + sum(widths[:i]), w) for i, w in enumerate(widths)]
 
 
 def tile_picked_wema_tanh_l_kernel(tc, x_words, x_scales, mem, w1, old, new, slot, out):
     nc = tc.nc
     with ExitStack() as ctx:
         keep = ctx.enter_context(tc.tile_pool(name="keep", bufs=1))
-        psum = ctx.enter_context(tc.psum_pool(name="psum", bufs=1))
+        psum = ctx.enter_context(tc.psum_pool(name="psum", bufs=8))
+
+        def bank(name):
+            return psum.tile([P, BANK], F32, tag="bank", name=name)
 
         x_plane = keep.tile([P, T], U8, align_bytes=64)
-        nc.vector.memset(x_plane[:].bitcast(I32), 0)
-        new_rows = keep.tile([P, P], F32)
-        nc.vector.memset(new_rows[:], 0.0)
+        nc.gpsimd.memset(x_plane[:].bitcast(I32), 0)
         warm_in = keep.tile([P, 1], F32)
         nc.vector.memset(warm_in[:], 0.0)
         warm_out = keep.tile([P, 1], F32)
         nc.scalar.activation(out=warm_out[:], in_=warm_in[:], func=ACT.Tanh)
         ident = keep.tile([P, P], F32)
-        make_identity(nc, ident[:])
+        zeros = keep.tile([P, P], F32, tag="x", align_bytes=64)
+        nc.gpsimd.memset(zeros[:], 0.0)
+        nc.gpsimd.affine_select(
+            out=ident[:],
+            in_=zeros[:],
+            compare_op=ALU.not_equal,
+            fill=1.0,
+            base=0,
+            pattern=[[-1, P]],
+            channel_multiplier=1,
+        )
+        gate_rows = keep.tile([P, P], F32)
+        nc.gpsimd.memset(gate_rows[32:64, :], 0.0)
+        nc.gpsimd.memset(gate_rows[64:P, :], 0.0)
 
         old_cols = keep.tile([P, BLOCKS], F32)
         nc.sync.dma_start(out=old_cols[:], in_=old[0:1, :].rearrange("o (n i) -> (o n) i", i=BLOCKS))
+        nc.sync.dma_start(out=gate_rows[0:32, :], in_=new[0:4, :].rearrange("r (b c) -> (r b) c", c=P))
         w_raw = keep.tile([P, PASSES, 4, N], F32)
         nc.sync.dma_start(out=w_raw[:], in_=w1.rearrange("(g p j) m -> p g j m", g=PASSES, j=4))
         offs = keep.tile([P, T // 16], U16)
         nc.sync.dma_start(out=offs[:], in_=slot)
         window = keep.tile([P, U], F32)
         nc.sync.dma_start(out=window[:], in_=mem)
-        nc.sync.dma_start(out=new_rows[0:BLOCKS, :], in_=new[0:1, :].rearrange("o (b c) -> (o b) c", c=P))
         for q in range(4):
             nc.sync.dma_start(
                 out=x_plane[32 * q : 32 * q + 4 * PASSES, :].bitcast(I32),
                 in_=x_scales[:, 4 * q : 4 * q + 4, :].bitcast(I32),
             )
-        x_tiles = []
-        c0 = 0
-        for ci, n in enumerate(CHUNKS):
-            xt = keep.tile([P, PASSES, n], U32, align_bytes=64, name=f"x{ci}")
+        x = keep.tile([P, PASSES * T], U32, tag="x", align_bytes=64)
+        for c0, n in spans(LOADS):
             nc.sync.dma_start(
-                out=xt[:].bitcast(I32),
+                out=x[:, PASSES * c0 : PASSES * (c0 + n)].rearrange("p (g n) -> p g n", g=PASSES).bitcast(I32),
                 in_=x_words[:, :, c0 : c0 + n, :].rearrange("g p n t -> p g (n t)").bitcast(I32),
             )
-            x_tiles.append(xt)
-            c0 = c0 + n
+
+        def x_cols(g, c0, n):
+            l0, ln = [span for span in spans(LOADS) if span[0] <= c0][-1]
+            start = PASSES * l0 + g * ln + c0 - l0
+            return x[:, start : start + n]
 
         w_grouped = keep.tile([P, PASSES, N, 4], BF16, align_bytes=64)
         nc.vector.tensor_copy(out=w_grouped[:], in_=w_raw[:].rearrange("p g j m -> p g m j"))
@@ -77,17 +100,11 @@ def tile_picked_wema_tanh_l_kernel(tc, x_words, x_scales, mem, w1, old, new, slo
 
         old_all = keep.tile([P, P, BLOCKS], F32)
         for h in range(2):
-            spread = psum.tile([P, 4, P], F32, name=f"spread{h}")
+            old_ps = bank(f"old_ps{h}")
             for i in range(4):
-                col = 4 * h + i
-                nc.tensor.transpose(spread[:, i, :], old_cols[:, col : col + 1].to_broadcast([P, P]), ident[:])
-            nc.scalar.copy(out=old_all[:, :, 4 * h : 4 * h + 4], in_=spread[:].rearrange("p i n -> p n i"))
-
-        new_ps = psum.tile([P, P], F32)
-        nc.tensor.transpose(new_ps[:], new_rows[:], ident[:])
-        new_cols = keep.tile([P, BLOCKS], F32)
-        nc.scalar.copy(out=new_cols[:], in_=new_ps[:, 0:BLOCKS])
-
+                col = old_cols[:, 4 * h + i : 4 * h + i + 1]
+                nc.tensor.transpose(old_ps[:, i * P : (i + 1) * P], col.to_broadcast([P, P]), ident[:])
+            nc.scalar.copy(out=old_all[:, :, 4 * h : 4 * h + 4], in_=old_ps[:].rearrange("p (i n) -> p n i", i=4))
         kept = keep.tile([P, T], F32)
         nc.vector.tensor_tensor(
             out=kept[:],
@@ -96,43 +113,77 @@ def tile_picked_wema_tanh_l_kernel(tc, x_words, x_scales, mem, w1, old, new, slo
             op=ALU.mult,
         )
 
-        c0 = 0
-        for ci, n in enumerate(CHUNKS):
-            xt = x_tiles[ci]
-            nb = n // P
-            acc = psum.tile([P, 512], F32, tag="acc", bufs=3, name=f"acc{ci}")
-            for b in range(nb):
+        gate_ps = bank("gate_ps")
+        nc.tensor.transpose(gate_ps[:, 0:P], gate_rows[:], ident[:])
+        gate_cols = keep.tile([P, BLOCKS], F32)
+        nc.scalar.copy(out=gate_cols[:], in_=gate_ps[:, 0:BLOCKS])
+        new_ps = bank("new_ps")
+        for b in range(HEAD // P):
+            nc.tensor.transpose(new_ps[:, b * P : (b + 1) * P], gate_cols[:, b : b + 1].to_broadcast([P, P]), ident[:])
+
+        fresh = keep.tile([P, T], F32)
+        y_head = keep.tile([P, HEAD], F32)
+        for c0, n in spans(HEAD_GROUPS):
+            acc = bank(f"acc{c0}")
+            for g in range(PASSES):
+                nc.tensor.matmul_mx(
+                    out=acc[:, 0:n],
+                    lhsT=w_codes[:, g * N : (g + 1) * N].bitcast(FP8X4),
+                    lhsT_scale=w_plane[:, g * N : (g + 1) * N],
+                    rhs=x_cols(g, c0, n).bitcast(FP8X4),
+                    rhs_scale=x_plane[4 * g : P, c0 : c0 + n],
+                    start=(g == 0),
+                    stop=(g == PASSES - 1),
+                )
+            nc.scalar.activation(out=y_head[:, c0 : c0 + n], in_=acc[:, 0:n], func=ACT.Tanh, bias=warm_out[:])
+        nc.vector.tensor_tensor(out=fresh[:, 0:HEAD], in0=y_head[:], in1=new_ps[:, 0:HEAD], op=ALU.mult)
+
+        y_tail = keep.tile([P, T - HEAD], F32)
+        z_tail = keep.tile([P, T - HEAD], F32)
+
+        def project(c0, n):
+            acc = bank(f"acc{c0}")
+            for b in range(n // P):
                 for g in range(PASSES):
                     nc.tensor.matmul_mx(
                         out=acc[:, b * P : (b + 1) * P],
-                        lhsT=xt[:, g, b * P : (b + 1) * P].bitcast(FP8X4),
+                        lhsT=x_cols(g, c0 + b * P, P).bitcast(FP8X4),
                         lhsT_scale=x_plane[4 * g : P, c0 + b * P : c0 + (b + 1) * P],
                         rhs=w_codes[:, g * N : (g + 1) * N].bitcast(FP8X4),
                         rhs_scale=w_plane[:, g * N : (g + 1) * N],
                         start=(g == 0),
                         stop=(g == PASSES - 1),
                     )
-            y_t = keep.tile([P, n], F32, name=f"y{ci}")
-            nc.scalar.activation(out=y_t[:], in_=acc[:, 0:n], func=ACT.Tanh)
-            z_t = keep.tile([P, n], F32, name=f"z{ci}")
-            back = psum.tile([P, 512], F32, tag="back", bufs=2, name=f"back{ci}")
-            for b in range(nb):
-                blk = c0 // P + b
+            nc.scalar.activation(out=y_tail[:, c0 - HEAD : c0 - HEAD + n], in_=acc[:, 0:n], func=ACT.Tanh, bias=warm_out[:])
+
+        def weigh_and_turn(c0, n):
+            back = bank(f"back{c0}")
+            for b in range(n // P):
+                cols = slice(c0 - HEAD + b * P, c0 - HEAD + (b + 1) * P)
+                col = c0 // P + b
                 nc.scalar.activation(
-                    out=z_t[:, b * P : (b + 1) * P],
-                    in_=y_t[:, b * P : (b + 1) * P],
-                    func=ACT.Copy,
-                    scale=new_cols[:, blk : blk + 1],
+                    out=z_tail[:, cols], in_=y_tail[:, cols], func=ACT.Copy, scale=gate_cols[:, col : col + 1]
                 )
-                nc.tensor.transpose(back[:, b * P : (b + 1) * P], z_t[:, b * P : (b + 1) * P], ident[:])
-            fresh = keep.tile([P, n], F32, name=f"fresh{ci}")
-            nc.scalar.copy(out=fresh[:], in_=back[:, 0:n])
+                nc.tensor.transpose(back[:, b * P : (b + 1) * P], z_tail[:, cols], ident[:])
+            return back
+
+        groups = spans(TAIL_GROUPS, HEAD)
+        backs = []
+        for step in range(len(groups) + 2):
+            if step < len(groups):
+                project(*groups[step])
+            if 1 <= step <= len(groups):
+                backs.append(weigh_and_turn(*groups[step - 1]))
+            if step >= 2:
+                c0, n = groups[step - 2]
+                nc.scalar.copy(out=fresh[:, c0 : c0 + n], in_=backs[step - 2][:, 0:n])
+
+        for c0, n in spans(SCATTERS):
             nc.vector.tensor_tensor(
                 out=window[:].indirect(offs[:, c0 // 16 : (c0 + n) // 16]),
                 in0=kept[:, c0 : c0 + n],
-                in1=fresh[:],
+                in1=fresh[:, c0 : c0 + n],
                 op=ALU.add,
             )
-            c0 = c0 + n
 
         nc.sync.dma_start(out=out, in_=window[:])

@@ -20,11 +20,11 @@ P = 128
 BANK = 512
 PASSES = K // 512
 BLOCKS = T // P
-HEAD_GROUPS = (256, 128)
-TAIL_GROUPS = (256, 256, 128)
-LOADS = (256, 128, 256, 384)
+HEAD_GROUPS = (256,)
+TAIL_GROUPS = (256, 256, 256)
+LOADS = (256, 256, 512)
 HEAD = sum(HEAD_GROUPS)
-SCATTERS = (384, 640)
+SCATTERS = (256, 256, 512)
 
 
 def spans(widths, start=0):
@@ -59,12 +59,10 @@ def tile_picked_wema_tanh_l_kernel(tc, x_words, x_scales, mem, w1, old, new, slo
             channel_multiplier=1,
         )
         gate_rows = keep.tile([P, P], F32)
-        nc.gpsimd.memset(gate_rows[32:64, :], 0.0)
         nc.gpsimd.memset(gate_rows[64:P, :], 0.0)
 
-        old_cols = keep.tile([P, BLOCKS], F32)
-        nc.sync.dma_start(out=old_cols[:], in_=old[0:1, :].rearrange("o (n i) -> (o n) i", i=BLOCKS))
-        nc.sync.dma_start(out=gate_rows[0:32, :], in_=new[0:4, :].rearrange("r (b c) -> (r b) c", c=P))
+        nc.sync.dma_start(out=gate_rows[0:32, :], in_=old[0:4, :].rearrange("r (b c) -> (r b) c", c=P))
+        nc.sync.dma_start(out=gate_rows[32:64, :], in_=new[0:4, :].rearrange("r (b c) -> (r b) c", c=P))
         w_raw = keep.tile([P, PASSES, 4, N], F32)
         nc.sync.dma_start(out=w_raw[:], in_=w1.rearrange("(g p j) m -> p g j m", g=PASSES, j=4))
         offs = keep.tile([P, T // 16], U16)
@@ -98,28 +96,26 @@ def tile_picked_wema_tanh_l_kernel(tc, x_words, x_scales, mem, w1, old, new, slo
             in_=w_grouped[:].rearrange("p g m j -> p (g m j)"),
         )
 
-        old_all = keep.tile([P, P, BLOCKS], F32)
-        for h in range(2):
-            old_ps = bank(f"old_ps{h}")
-            for i in range(4):
-                col = old_cols[:, 4 * h + i : 4 * h + i + 1]
-                nc.tensor.transpose(old_ps[:, i * P : (i + 1) * P], col.to_broadcast([P, P]), ident[:])
-            nc.scalar.copy(out=old_all[:, :, 4 * h : 4 * h + 4], in_=old_ps[:].rearrange("p (i n) -> p n i", i=4))
-        kept = keep.tile([P, T], F32)
-        nc.vector.tensor_tensor(
-            out=kept[:],
-            in0=window[:].indirect(offs[:]),
-            in1=old_all[:].rearrange("p n i -> p (n i)"),
-            op=ALU.mult,
-        )
-
         gate_ps = bank("gate_ps")
         nc.tensor.transpose(gate_ps[:, 0:P], gate_rows[:], ident[:])
-        gate_cols = keep.tile([P, BLOCKS], F32)
-        nc.scalar.copy(out=gate_cols[:], in_=gate_ps[:, 0:BLOCKS])
+        gate_cols = keep.tile([P, 2, BLOCKS], F32)
+        nc.scalar.copy(out=gate_cols[:], in_=gate_ps[:, 0:64].rearrange("p (v r) -> p v r", v=2)[:, :, 0:BLOCKS])
+
+        def spread(dst, vec, first_block, blocks):
+            for b in range(blocks):
+                col = gate_cols[:, vec, first_block + b : first_block + b + 1]
+                nc.tensor.transpose(dst[:, b * P : (b + 1) * P], col.to_broadcast([P, P]), ident[:])
+
+        old_all = keep.tile([P, T], F32)
+        for c0, n in spans((BANK, BANK)):
+            old_ps = bank(f"old_ps{c0}")
+            spread(old_ps, 0, c0 // P, n // P)
+            nc.scalar.copy(out=old_all[:, c0 : c0 + n], in_=old_ps[:])
         new_ps = bank("new_ps")
-        for b in range(HEAD // P):
-            nc.tensor.transpose(new_ps[:, b * P : (b + 1) * P], gate_cols[:, b : b + 1].to_broadcast([P, P]), ident[:])
+        spread(new_ps, 1, 0, HEAD // P)
+
+        kept = keep.tile([P, T], F32)
+        nc.vector.tensor_tensor(out=kept[:], in0=window[:].indirect(offs[:]), in1=old_all[:], op=ALU.mult)
 
         fresh = keep.tile([P, T], F32)
         y_head = keep.tile([P, HEAD], F32)
@@ -162,7 +158,7 @@ def tile_picked_wema_tanh_l_kernel(tc, x_words, x_scales, mem, w1, old, new, slo
                 cols = slice(c0 - HEAD + b * P, c0 - HEAD + (b + 1) * P)
                 col = c0 // P + b
                 nc.scalar.activation(
-                    out=z_tail[:, cols], in_=y_tail[:, cols], func=ACT.Copy, scale=gate_cols[:, col : col + 1]
+                    out=z_tail[:, cols], in_=y_tail[:, cols], func=ACT.Copy, scale=gate_cols[:, 1, col : col + 1]
                 )
                 nc.tensor.transpose(back[:, b * P : (b + 1) * P], z_tail[:, cols], ident[:])
             return back

@@ -20,11 +20,12 @@ P = 128
 BANK = 512
 PASSES = K // 512
 BLOCKS = T // P
-HEAD_GROUPS = (256,)
-TAIL_GROUPS = (256, 256, 256)
+HEAD_GROUPS = (128, 128, 128)
+HEAD_PRODUCTS = (256, 128)
+TAIL_GROUPS = (128, 256, 256)
 LOADS = (256, 256, 512)
 HEAD = sum(HEAD_GROUPS)
-SCATTERS = (256, 256, 512)
+SCATTERS = (384, 640)
 
 
 def spans(widths, start=0):
@@ -61,19 +62,22 @@ def tile_picked_wema_tanh_l_kernel(tc, x_words, x_scales, mem, w1, old, new, slo
         gate_rows = keep.tile([P, P], F32)
         nc.gpsimd.memset(gate_rows[64:P, :], 0.0)
 
+        w_rows = w1.rearrange("(g p j) m -> g p j m", g=PASSES, j=4)
+        w_raw = [keep.tile([P, 4, N], F32, name=f"w_raw{g}") for g in range(PASSES)]
+        nc.sync.dma_start(out=w_raw[0][:], in_=w_rows[0])
         nc.sync.dma_start(out=gate_rows[0:32, :], in_=old[0:4, :].rearrange("r (b c) -> (r b) c", c=P))
         nc.sync.dma_start(out=gate_rows[32:64, :], in_=new[0:4, :].rearrange("r (b c) -> (r b) c", c=P))
-        w_raw = keep.tile([P, PASSES, 4, N], F32)
-        nc.sync.dma_start(out=w_raw[:], in_=w1.rearrange("(g p j) m -> p g j m", g=PASSES, j=4))
+        nc.sync.dma_start(out=w_raw[1][:], in_=w_rows[1])
         offs = keep.tile([P, T // 16], U16)
         nc.sync.dma_start(out=offs[:], in_=slot)
         window = keep.tile([P, U], F32)
         nc.sync.dma_start(out=window[:], in_=mem)
-        for q in range(4):
-            nc.sync.dma_start(
-                out=x_plane[32 * q : 32 * q + 4 * PASSES, :].bitcast(I32),
-                in_=x_scales[:, 4 * q : 4 * q + 4, :].bitcast(I32),
-            )
+        for engine, (c0, n) in zip((nc.sync,), spans((T,))):
+            for q in range(4):
+                engine.dma_start(
+                    out=x_plane[32 * q : 32 * q + 4 * PASSES, c0 : c0 + n].bitcast(I32),
+                    in_=x_scales[:, 4 * q : 4 * q + 4, c0 : c0 + n].bitcast(I32),
+                )
         x = keep.tile([P, PASSES * T], U32, tag="x", align_bytes=64)
         for c0, n in spans(LOADS):
             nc.sync.dma_start(
@@ -87,7 +91,8 @@ def tile_picked_wema_tanh_l_kernel(tc, x_words, x_scales, mem, w1, old, new, slo
             return x[:, start : start + n]
 
         w_grouped = keep.tile([P, PASSES, N, 4], BF16, align_bytes=64)
-        nc.vector.tensor_copy(out=w_grouped[:], in_=w_raw[:].rearrange("p g j m -> p g m j"))
+        for g in range(PASSES):
+            nc.vector.tensor_copy(out=w_grouped[:, g], in_=w_raw[g][:].rearrange("p j m -> p m j"))
         w_codes = keep.tile([P, PASSES * N], U32, align_bytes=64)
         w_plane = keep.tile([P, PASSES * N], U8, align_bytes=64)
         nc.vector.quantize_mx(
@@ -107,15 +112,21 @@ def tile_picked_wema_tanh_l_kernel(tc, x_words, x_scales, mem, w1, old, new, slo
                 nc.tensor.transpose(dst[:, b * P : (b + 1) * P], col.to_broadcast([P, P]), ident[:])
 
         old_all = keep.tile([P, T], F32)
-        for c0, n in spans((BANK, BANK)):
+        for copy, (c0, n) in zip((nc.vector.tensor_copy, nc.scalar.copy), spans((BANK, BANK))):
             old_ps = bank(f"old_ps{c0}")
             spread(old_ps, 0, c0 // P, n // P)
-            nc.scalar.copy(out=old_all[:, c0 : c0 + n], in_=old_ps[:])
+            copy(out=old_all[:, c0 : c0 + n], in_=old_ps[:])
         new_ps = bank("new_ps")
         spread(new_ps, 1, 0, HEAD // P)
 
         kept = keep.tile([P, T], F32)
-        nc.vector.tensor_tensor(out=kept[:], in0=window[:].indirect(offs[:]), in1=old_all[:], op=ALU.mult)
+        for c0, n in spans((BANK, BANK)):
+            nc.vector.tensor_tensor(
+                out=kept[:, c0 : c0 + n],
+                in0=window[:].indirect(offs[:, c0 // 16 : (c0 + n) // 16]),
+                in1=old_all[:, c0 : c0 + n],
+                op=ALU.mult,
+            )
 
         fresh = keep.tile([P, T], F32)
         y_head = keep.tile([P, HEAD], F32)
@@ -132,7 +143,10 @@ def tile_picked_wema_tanh_l_kernel(tc, x_words, x_scales, mem, w1, old, new, slo
                     stop=(g == PASSES - 1),
                 )
             nc.scalar.activation(out=y_head[:, c0 : c0 + n], in_=acc[:, 0:n], func=ACT.Tanh, bias=warm_out[:])
-        nc.vector.tensor_tensor(out=fresh[:, 0:HEAD], in0=y_head[:], in1=new_ps[:, 0:HEAD], op=ALU.mult)
+        for c0, n in spans(HEAD_PRODUCTS):
+            nc.vector.tensor_tensor(
+                out=fresh[:, c0 : c0 + n], in0=y_head[:, c0 : c0 + n], in1=new_ps[:, c0 : c0 + n], op=ALU.mult
+            )
 
         y_tail = keep.tile([P, T - HEAD], F32)
         z_tail = keep.tile([P, T - HEAD], F32)

@@ -20,9 +20,9 @@ P = 128
 BANK = 512
 PASSES = K // 512
 BLOCKS = T // P
-HEAD_GROUPS = (128, 128, 128)
-HEAD_PRODUCTS = (256, 128)
-TAIL_GROUPS = (128, 256, 256)
+HEAD_GROUPS = (128, 128, 128, 128)
+HEAD_PRODUCTS = (256, 128, 128)
+TAIL_GROUPS = (256, 256)
 LOADS = (256, 256, 512)
 HEAD = sum(HEAD_GROUPS)
 SCATTERS = (384, 640)
@@ -42,7 +42,7 @@ def tile_picked_wema_tanh_l_kernel(tc, x_words, x_scales, mem, w1, old, new, slo
             return psum.tile([P, BANK], F32, tag="bank", name=name)
 
         x_plane = keep.tile([P, T], U8, align_bytes=64)
-        nc.gpsimd.memset(x_plane[:].bitcast(I32), 0)
+        nc.vector.memset(x_plane[:].bitcast(I32), 0)
         warm_in = keep.tile([P, 1], F32)
         nc.vector.memset(warm_in[:], 0.0)
         warm_out = keep.tile([P, 1], F32)
@@ -60,7 +60,7 @@ def tile_picked_wema_tanh_l_kernel(tc, x_words, x_scales, mem, w1, old, new, slo
             channel_multiplier=1,
         )
         gate_rows = keep.tile([P, P], F32)
-        nc.gpsimd.memset(gate_rows[64:P, :], 0.0)
+        nc.vector.memset(gate_rows[64:P, :], 0.0)
 
         w_rows = w1.rearrange("(g p j) m -> g p j m", g=PASSES, j=4)
         w_raw = [keep.tile([P, 4, N], F32, name=f"w_raw{g}") for g in range(PASSES)]
@@ -72,7 +72,7 @@ def tile_picked_wema_tanh_l_kernel(tc, x_words, x_scales, mem, w1, old, new, slo
         nc.sync.dma_start(out=offs[:], in_=slot)
         window = keep.tile([P, U], F32)
         nc.sync.dma_start(out=window[:], in_=mem)
-        for engine, (c0, n) in zip((nc.sync,), spans((T,))):
+        for engine, (c0, n) in zip((nc.sync, nc.gpsimd), spans((BANK, BANK))):
             for q in range(4):
                 engine.dma_start(
                     out=x_plane[32 * q : 32 * q + 4 * PASSES, c0 : c0 + n].bitcast(I32),

@@ -42,7 +42,15 @@ def tile_picked_wema_tanh_l_kernel(tc, x_words, x_scales, mem, w1, old, new, slo
             return psum.tile([P, BANK], F32, tag="bank", name=name)
 
         x_plane = keep.tile([P, T], U8, align_bytes=64)
-        nc.vector.memset(x_plane[:].bitcast(I32), 0)
+        nc.gpsimd.memset(x_plane[:].bitcast(I32), 0)
+
+        def load_scales(engine, q, c0, n):
+            engine.dma_start(
+                out=x_plane[32 * q : 32 * q + 4 * PASSES, c0 : c0 + n].bitcast(I32),
+                in_=x_scales[:, 4 * q : 4 * q + 4, c0 : c0 + n].bitcast(I32),
+            )
+
+        load_scales(nc.gpsimd, 0, BANK, BANK)
         warm_in = keep.tile([P, 1], F32)
         nc.vector.memset(warm_in[:], 0.0)
         warm_out = keep.tile([P, 1], F32)
@@ -72,12 +80,11 @@ def tile_picked_wema_tanh_l_kernel(tc, x_words, x_scales, mem, w1, old, new, slo
         nc.sync.dma_start(out=offs[:], in_=slot)
         window = keep.tile([P, U], F32)
         nc.sync.dma_start(out=window[:], in_=mem)
-        for engine, (c0, n) in zip((nc.sync, nc.gpsimd), spans((BANK, BANK))):
-            for q in range(4):
-                engine.dma_start(
-                    out=x_plane[32 * q : 32 * q + 4 * PASSES, c0 : c0 + n].bitcast(I32),
-                    in_=x_scales[:, 4 * q : 4 * q + 4, c0 : c0 + n].bitcast(I32),
-                )
+        for q in range(3):
+            load_scales(nc.sync, q, 0, BANK)
+        load_scales(nc.sync, 3, 0, T)
+        for q in range(1, 3):
+            load_scales(nc.gpsimd, q, BANK, BANK)
         x = keep.tile([P, PASSES * T], U32, tag="x", align_bytes=64)
         for c0, n in spans(LOADS):
             nc.sync.dma_start(

@@ -19,12 +19,16 @@ ALU = mybir.AluOpType
 P = 128
 BANK = 512
 PASSES = K // 512
+QUADRANTS = 4
 BLOCKS = T // P
+HEAD = BANK
+
+X_LOADS = (256, 256, 512)
+OLD_COPIES = (256, 256, 512)
+GATHERS = (512, 512)
 HEAD_GROUPS = (128, 128, 128, 128)
 HEAD_PRODUCTS = (256, 128, 128)
 TAIL_GROUPS = (256, 256)
-LOADS = (256, 256, 512)
-HEAD = sum(HEAD_GROUPS)
 SCATTERS = (384, 640)
 
 
@@ -41,93 +45,93 @@ def tile_picked_wema_tanh_l_kernel(tc, x_words, x_scales, mem, w1, old, new, slo
         def bank(name):
             return psum.tile([P, BANK], F32, tag="bank", name=name)
 
-        x_plane = keep.tile([P, T], U8, align_bytes=64)
-        nc.gpsimd.memset(x_plane[:].bitcast(I32), 0)
-
-        def load_scales(engine, q, c0, n):
-            engine.dma_start(
-                out=x_plane[32 * q : 32 * q + 4 * PASSES, c0 : c0 + n].bitcast(I32),
-                in_=x_scales[:, 4 * q : 4 * q + 4, c0 : c0 + n].bitcast(I32),
-            )
-
-        load_scales(nc.gpsimd, 0, BANK, BANK)
-        warm_in = keep.tile([P, 1], F32)
-        nc.vector.memset(warm_in[:], 0.0)
-        warm_out = keep.tile([P, 1], F32)
-        nc.scalar.activation(out=warm_out[:], in_=warm_in[:], func=ACT.Tanh)
+        gate_rows = keep.tile([P, P], F32)
+        nc.gpsimd.memset(gate_rows[:], 0.0)
+        head_plane = keep.tile([P, HEAD], U8, align_bytes=64)
+        nc.gpsimd.memset(head_plane[:].bitcast(I32), 0)
+        zero_in = keep.tile([P, 1], F32, tag="x", align_bytes=64)
+        nc.vector.memset(zero_in[:], 0.0)
+        zero_bias = keep.tile([P, 1], F32)
+        nc.scalar.activation(out=zero_bias[:], in_=zero_in[:], func=ACT.Tanh)
         ident = keep.tile([P, P], F32)
-        zeros = keep.tile([P, P], F32, tag="x", align_bytes=64)
-        nc.gpsimd.memset(zeros[:], 0.0)
+        ident_zeros = keep.tile([P, P], F32, tag="tail_plane", align_bytes=64)
+        nc.gpsimd.memset(ident_zeros[:], 0.0)
         nc.gpsimd.affine_select(
             out=ident[:],
-            in_=zeros[:],
+            in_=ident_zeros[:],
             compare_op=ALU.not_equal,
             fill=1.0,
             base=0,
             pattern=[[-1, P]],
             channel_multiplier=1,
         )
-        gate_rows = keep.tile([P, P], F32)
-        nc.vector.memset(gate_rows[64:P, :], 0.0)
+        tail_plane = keep.tile([P, T - HEAD], U8, tag="tail_plane", align_bytes=64)
+        nc.gpsimd.memset(tail_plane[:].bitcast(I32), 0)
 
         w_rows = w1.rearrange("(g p j) m -> g p j m", g=PASSES, j=4)
         w_raw = [keep.tile([P, 4, N], F32, name=f"w_raw{g}") for g in range(PASSES)]
         nc.sync.dma_start(out=w_raw[0][:], in_=w_rows[0])
-        nc.sync.dma_start(out=gate_rows[0:32, :], in_=old[0:4, :].rearrange("r (b c) -> (r b) c", c=P))
-        nc.sync.dma_start(out=gate_rows[32:64, :], in_=new[0:4, :].rearrange("r (b c) -> (r b) c", c=P))
-        nc.sync.dma_start(out=w_raw[1][:], in_=w_rows[1])
         offs = keep.tile([P, T // 16], U16)
         nc.sync.dma_start(out=offs[:], in_=slot)
+        nc.sync.dma_start(out=gate_rows[0:BLOCKS, :], in_=old[0, :].rearrange("(b c) -> b c", c=P))
+        nc.sync.dma_start(out=gate_rows[BLOCKS : 2 * BLOCKS, :], in_=new[0, :].rearrange("(b c) -> b c", c=P))
+        nc.sync.dma_start(out=w_raw[1][:], in_=w_rows[1])
         window = keep.tile([P, U], F32)
         nc.sync.dma_start(out=window[:], in_=mem)
-        for q in range(3):
-            load_scales(nc.sync, q, 0, BANK)
-        load_scales(nc.sync, 3, 0, T)
-        for q in range(1, 3):
-            load_scales(nc.gpsimd, q, BANK, BANK)
+
+        def load_scales(engine, plane, q, c0, n):
+            engine.dma_start(
+                out=plane[32 * q : 32 * q + 4 * PASSES, :].bitcast(I32),
+                in_=x_scales[:, 4 * q : 4 * q + 4, c0 : c0 + n].bitcast(I32),
+            )
+
+        for q in range(QUADRANTS):
+            load_scales(nc.sync, head_plane, q, 0, HEAD)
         x = keep.tile([P, PASSES * T], U32, tag="x", align_bytes=64)
-        for c0, n in spans(LOADS):
+        for c0, n in spans(X_LOADS):
             nc.sync.dma_start(
                 out=x[:, PASSES * c0 : PASSES * (c0 + n)].rearrange("p (g n) -> p g n", g=PASSES).bitcast(I32),
                 in_=x_words[:, :, c0 : c0 + n, :].rearrange("g p n t -> p g (n t)").bitcast(I32),
             )
+        for q, engine in enumerate((nc.gpsimd, nc.gpsimd, nc.sync, nc.sync)):
+            load_scales(engine, tail_plane, q, HEAD, T - HEAD)
 
-        def x_cols(g, c0, n):
-            l0, ln = [span for span in spans(LOADS) if span[0] <= c0][-1]
-            start = PASSES * l0 + g * ln + c0 - l0
-            return x[:, start : start + n]
+        def x_codes(g, c0, n):
+            load0, width = [span for span in spans(X_LOADS) if span[0] <= c0][-1]
+            start = PASSES * load0 + g * width + c0 - load0
+            return x[:, start : start + n].bitcast(FP8X4)
 
         w_grouped = keep.tile([P, PASSES, N, 4], BF16, align_bytes=64)
         for g in range(PASSES):
             nc.vector.tensor_copy(out=w_grouped[:, g], in_=w_raw[g][:].rearrange("p j m -> p m j"))
-        w_codes = keep.tile([P, PASSES * N], U32, align_bytes=64)
+        w_words = keep.tile([P, PASSES * N], U32, align_bytes=64)
         w_plane = keep.tile([P, PASSES * N], U8, align_bytes=64)
         nc.vector.quantize_mx(
-            out=w_codes[:].bitcast(FP8X4),
+            out=w_words[:].bitcast(FP8X4),
             scales=w_plane[:],
             in_=w_grouped[:].rearrange("p g m j -> p (g m j)"),
         )
 
-        gate_ps = bank("gate_ps")
-        nc.tensor.transpose(gate_ps[:, 0:P], gate_rows[:], ident[:])
+        gate_turned = bank("gate_turned")
+        nc.tensor.transpose(gate_turned[:, 0:P], gate_rows[:], ident[:])
         gate_cols = keep.tile([P, 2, BLOCKS], F32)
-        nc.scalar.copy(out=gate_cols[:], in_=gate_ps[:, 0:64].rearrange("p (v r) -> p v r", v=2)[:, :, 0:BLOCKS])
+        nc.scalar.copy(out=gate_cols[:], in_=gate_turned[:, 0 : 2 * BLOCKS].rearrange("p (v b) -> p v b", v=2))
 
-        def spread(dst, vec, first_block, blocks):
-            for b in range(blocks):
-                col = gate_cols[:, vec, first_block + b : first_block + b + 1]
+        def spread(dst, v, c0, n):
+            for b in range(n // P):
+                col = gate_cols[:, v, c0 // P + b : c0 // P + b + 1]
                 nc.tensor.transpose(dst[:, b * P : (b + 1) * P], col.to_broadcast([P, P]), ident[:])
 
         old_all = keep.tile([P, T], F32)
-        for copy, (c0, n) in zip((nc.vector.tensor_copy, nc.scalar.copy), spans((BANK, BANK))):
-            old_ps = bank(f"old_ps{c0}")
-            spread(old_ps, 0, c0 // P, n // P)
-            copy(out=old_all[:, c0 : c0 + n], in_=old_ps[:])
-        new_ps = bank("new_ps")
-        spread(new_ps, 1, 0, HEAD // P)
+        for copy, (c0, n) in zip((nc.scalar.copy, nc.vector.tensor_copy, nc.scalar.copy), spans(OLD_COPIES)):
+            old_spread = bank(f"old_spread{c0}")
+            spread(old_spread, 0, c0, n)
+            copy(out=old_all[:, c0 : c0 + n], in_=old_spread[:, 0:n])
+        new_spread = bank("new_spread")
+        spread(new_spread, 1, 0, HEAD)
 
         kept = keep.tile([P, T], F32)
-        for c0, n in spans((BANK, BANK)):
+        for c0, n in spans(GATHERS):
             nc.vector.tensor_tensor(
                 out=kept[:, c0 : c0 + n],
                 in0=window[:].indirect(offs[:, c0 // 16 : (c0 + n) // 16]),
@@ -142,58 +146,48 @@ def tile_picked_wema_tanh_l_kernel(tc, x_words, x_scales, mem, w1, old, new, slo
             for g in range(PASSES):
                 nc.tensor.matmul_mx(
                     out=acc[:, 0:n],
-                    lhsT=w_codes[:, g * N : (g + 1) * N].bitcast(FP8X4),
+                    lhsT=w_words[:, g * N : (g + 1) * N].bitcast(FP8X4),
                     lhsT_scale=w_plane[:, g * N : (g + 1) * N],
-                    rhs=x_cols(g, c0, n).bitcast(FP8X4),
-                    rhs_scale=x_plane[4 * g : P, c0 : c0 + n],
+                    rhs=x_codes(g, c0, n),
+                    rhs_scale=head_plane[4 * g : P, c0 : c0 + n],
                     start=(g == 0),
                     stop=(g == PASSES - 1),
                 )
-            nc.scalar.activation(out=y_head[:, c0 : c0 + n], in_=acc[:, 0:n], func=ACT.Tanh, bias=warm_out[:])
+            nc.scalar.activation(out=y_head[:, c0 : c0 + n], in_=acc[:, 0:n], func=ACT.Tanh, bias=zero_bias[:])
         for c0, n in spans(HEAD_PRODUCTS):
             nc.vector.tensor_tensor(
-                out=fresh[:, c0 : c0 + n], in0=y_head[:, c0 : c0 + n], in1=new_ps[:, c0 : c0 + n], op=ALU.mult
+                out=fresh[:, c0 : c0 + n], in0=y_head[:, c0 : c0 + n], in1=new_spread[:, c0 : c0 + n], op=ALU.mult
             )
 
         y_tail = keep.tile([P, T - HEAD], F32)
-        z_tail = keep.tile([P, T - HEAD], F32)
-
-        def project(c0, n):
-            acc = bank(f"acc{c0}")
+        weighed = keep.tile([P, T - HEAD], F32)
+        for t0, n in spans(TAIL_GROUPS):
+            acc = bank(f"acc{HEAD + t0}")
             for b in range(n // P):
                 for g in range(PASSES):
                     nc.tensor.matmul_mx(
                         out=acc[:, b * P : (b + 1) * P],
-                        lhsT=x_cols(g, c0 + b * P, P).bitcast(FP8X4),
-                        lhsT_scale=x_plane[4 * g : P, c0 + b * P : c0 + (b + 1) * P],
-                        rhs=w_codes[:, g * N : (g + 1) * N].bitcast(FP8X4),
+                        lhsT=x_codes(g, HEAD + t0 + b * P, P),
+                        lhsT_scale=tail_plane[4 * g : P, t0 + b * P : t0 + (b + 1) * P],
+                        rhs=w_words[:, g * N : (g + 1) * N].bitcast(FP8X4),
                         rhs_scale=w_plane[:, g * N : (g + 1) * N],
                         start=(g == 0),
                         stop=(g == PASSES - 1),
                     )
-            nc.scalar.activation(out=y_tail[:, c0 - HEAD : c0 - HEAD + n], in_=acc[:, 0:n], func=ACT.Tanh, bias=warm_out[:])
-
-        def weigh_and_turn(c0, n):
-            back = bank(f"back{c0}")
+            nc.scalar.activation(out=y_tail[:, t0 : t0 + n], in_=acc[:, 0:n], func=ACT.Tanh, bias=zero_bias[:])
+        turned = []
+        for t0, n in spans(TAIL_GROUPS):
+            back = bank(f"back{t0}")
             for b in range(n // P):
-                cols = slice(c0 - HEAD + b * P, c0 - HEAD + (b + 1) * P)
-                col = c0 // P + b
+                cols = slice(t0 + b * P, t0 + (b + 1) * P)
+                block = (HEAD + t0) // P + b
                 nc.scalar.activation(
-                    out=z_tail[:, cols], in_=y_tail[:, cols], func=ACT.Copy, scale=gate_cols[:, 1, col : col + 1]
+                    out=weighed[:, cols], in_=y_tail[:, cols], func=ACT.Copy, scale=gate_cols[:, 1, block : block + 1]
                 )
-                nc.tensor.transpose(back[:, b * P : (b + 1) * P], z_tail[:, cols], ident[:])
-            return back
-
-        groups = spans(TAIL_GROUPS, HEAD)
-        backs = []
-        for step in range(len(groups) + 2):
-            if step < len(groups):
-                project(*groups[step])
-            if 1 <= step <= len(groups):
-                backs.append(weigh_and_turn(*groups[step - 1]))
-            if step >= 2:
-                c0, n = groups[step - 2]
-                nc.scalar.copy(out=fresh[:, c0 : c0 + n], in_=backs[step - 2][:, 0:n])
+                nc.tensor.transpose(back[:, b * P : (b + 1) * P], weighed[:, cols], ident[:])
+            turned.append(back)
+        for back, (t0, n) in zip(turned, spans(TAIL_GROUPS)):
+            nc.scalar.copy(out=fresh[:, HEAD + t0 : HEAD + t0 + n], in_=back[:, 0:n])
 
         for c0, n in spans(SCATTERS):
             nc.vector.tensor_tensor(

@@ -29,7 +29,7 @@ GATHERS = (512, 512)
 HEAD_GROUPS = (128, 128, 128, 128)
 HEAD_PRODUCTS = (256, 128, 128)
 TAIL_GROUPS = (256, 256)
-SCATTERS = (384, 640)
+SCATTERS = (512, 512)
 
 
 def spans(widths, start=0):

@@ -27,9 +27,9 @@ X_LOADS = (256, 256, 512)
 OLD_COPIES = (256, 256, 512)
 GATHERS = (512, 512)
 HEAD_GROUPS = (128, 128, 128, 128)
-HEAD_PRODUCTS = (256, 128, 128)
-TAIL_GROUPS = (256, 256)
-SCATTERS = (512, 512)
+HEAD_PRODUCTS = (256, 128, 64, 64)
+TAIL_GROUPS = (128, 256, 128)
+SCATTERS = (448, 576)
 
 
 def spans(widths, start=0):

@@ -23,11 +23,10 @@ QUADRANTS = 4
 BLOCKS = T // P
 HEAD = BANK
 
-X_LOADS = (256, 256, 512)
 OLD_COPIES = (256, 256, 512)
 GATHERS = (512, 512)
 HEAD_GROUPS = (128, 128, 128, 128)
-HEAD_PRODUCTS = (256, 128, 64, 64)
+HEAD_PRODUCTS = (128, 128, 128, 64, 64)
 TAIL_GROUPS = (128, 256, 128)
 SCATTERS = (448, 576)
 
@@ -47,7 +46,7 @@ def tile_picked_wema_tanh_l_kernel(tc, x_words, x_scales, mem, w1, old, new, slo
 
         gate_rows = keep.tile([P, P], F32)
         nc.gpsimd.memset(gate_rows[:], 0.0)
-        head_plane = keep.tile([P, HEAD], U8, align_bytes=64)
+        head_plane = keep.tile([P, PASSES, HEAD], U8, align_bytes=64)
         nc.gpsimd.memset(head_plane[:].bitcast(I32), 0)
         zero_in = keep.tile([P, 1], F32, tag="x", align_bytes=64)
         nc.vector.memset(zero_in[:], 0.0)
@@ -65,7 +64,7 @@ def tile_picked_wema_tanh_l_kernel(tc, x_words, x_scales, mem, w1, old, new, slo
             pattern=[[-1, P]],
             channel_multiplier=1,
         )
-        tail_plane = keep.tile([P, T - HEAD], U8, tag="tail_plane", align_bytes=64)
+        tail_plane = keep.tile([P, PASSES, T - HEAD], U8, tag="tail_plane", align_bytes=64)
         nc.gpsimd.memset(tail_plane[:].bitcast(I32), 0)
 
         w_rows = w1.rearrange("(g p j) m -> g p j m", g=PASSES, j=4)
@@ -81,25 +80,22 @@ def tile_picked_wema_tanh_l_kernel(tc, x_words, x_scales, mem, w1, old, new, slo
 
         def load_scales(engine, plane, q, c0, n):
             engine.dma_start(
-                out=plane[32 * q : 32 * q + 4 * PASSES, :].bitcast(I32),
-                in_=x_scales[:, 4 * q : 4 * q + 4, c0 : c0 + n].bitcast(I32),
+                out=plane[32 * q : 32 * q + 4].bitcast(I32),
+                in_=x_scales[:, 4 * q : 4 * q + 4, c0 : c0 + n].bitcast(I32).rearrange("g r n -> r g n"),
             )
 
         for q in range(QUADRANTS):
             load_scales(nc.sync, head_plane, q, 0, HEAD)
-        x = keep.tile([P, PASSES * T], U32, tag="x", align_bytes=64)
-        for c0, n in spans(X_LOADS):
-            nc.sync.dma_start(
-                out=x[:, PASSES * c0 : PASSES * (c0 + n)].rearrange("p (g n) -> p g n", g=PASSES).bitcast(I32),
-                in_=x_words[:, :, c0 : c0 + n, :].rearrange("g p n t -> p g (n t)").bitcast(I32),
-            )
+        x = keep.tile([P, 2, PASSES, HEAD], U32, tag="x", align_bytes=64)
+        x_rows = x_words.rearrange("g p n t -> p g (n t)").bitcast(I32)
+        for g in range(PASSES):
+            nc.sync.dma_start(out=x[:, 0, g, :].bitcast(I32), in_=x_rows[:, g, 0:HEAD])
+        nc.sync.dma_start(out=x[:, 1].bitcast(I32), in_=x_rows[:, :, HEAD:T])
         for q, engine in enumerate((nc.gpsimd, nc.gpsimd, nc.sync, nc.sync)):
             load_scales(engine, tail_plane, q, HEAD, T - HEAD)
 
         def x_codes(g, c0, n):
-            load0, width = [span for span in spans(X_LOADS) if span[0] <= c0][-1]
-            start = PASSES * load0 + g * width + c0 - load0
-            return x[:, start : start + n].bitcast(FP8X4)
+            return x[:, c0 // HEAD, g, c0 % HEAD : c0 % HEAD + n].bitcast(FP8X4)
 
         w_grouped = keep.tile([P, PASSES, N, 4], BF16, align_bytes=64)
         for g in range(PASSES):
@@ -141,18 +137,19 @@ def tile_picked_wema_tanh_l_kernel(tc, x_words, x_scales, mem, w1, old, new, slo
 
         fresh = keep.tile([P, T], F32)
         y_head = keep.tile([P, HEAD], F32)
-        for c0, n in spans(HEAD_GROUPS):
-            acc = bank(f"acc{c0}")
-            for g in range(PASSES):
+        accs = [bank(f"acc{c0}") for c0, n in spans(HEAD_GROUPS)]
+        for g in range(PASSES):
+            for acc, (c0, n) in zip(accs, spans(HEAD_GROUPS)):
                 nc.tensor.matmul_mx(
                     out=acc[:, 0:n],
                     lhsT=w_words[:, g * N : (g + 1) * N].bitcast(FP8X4),
                     lhsT_scale=w_plane[:, g * N : (g + 1) * N],
                     rhs=x_codes(g, c0, n),
-                    rhs_scale=head_plane[4 * g : P, c0 : c0 + n],
+                    rhs_scale=head_plane[:, g, c0 : c0 + n],
                     start=(g == 0),
                     stop=(g == PASSES - 1),
                 )
+        for acc, (c0, n) in zip(accs, spans(HEAD_GROUPS)):
             nc.scalar.activation(out=y_head[:, c0 : c0 + n], in_=acc[:, 0:n], func=ACT.Tanh, bias=zero_bias[:])
         for c0, n in spans(HEAD_PRODUCTS):
             nc.vector.tensor_tensor(
@@ -168,7 +165,7 @@ def tile_picked_wema_tanh_l_kernel(tc, x_words, x_scales, mem, w1, old, new, slo
                     nc.tensor.matmul_mx(
                         out=acc[:, b * P : (b + 1) * P],
                         lhsT=x_codes(g, HEAD + t0 + b * P, P),
-                        lhsT_scale=tail_plane[4 * g : P, t0 + b * P : t0 + (b + 1) * P],
+                        lhsT_scale=tail_plane[:, g, t0 + b * P : t0 + (b + 1) * P],
                         rhs=w_words[:, g * N : (g + 1) * N].bitcast(FP8X4),
                         rhs_scale=w_plane[:, g * N : (g + 1) * N],
                         start=(g == 0),

@@ -22,13 +22,13 @@ PASSES = K // 512
 QUADRANTS = 4
 BLOCKS = T // P
 HEAD = BANK
-
-OLD_COPIES = (256, 256, 512)
-GATHERS = (512, 512)
-HEAD_GROUPS = (128, 128, 128, 128)
-HEAD_PRODUCTS = (128, 128, 128, 64, 64)
+TAIL = T - HEAD
+FUSED = HEAD
+FIRST = P
+LATE = 256
+X_LOADS = (256, 256, 512)
+HEAD_GROUPS = (128, 128, 256)
 TAIL_GROUPS = (128, 256, 128)
-SCATTERS = (448, 576)
 
 
 def spans(widths, start=0):
@@ -39,12 +39,12 @@ def tile_picked_wema_tanh_l_kernel(tc, x_words, x_scales, mem, w1, old, new, slo
     nc = tc.nc
     with ExitStack() as ctx:
         keep = ctx.enter_context(tc.tile_pool(name="keep", bufs=1))
-        psum = ctx.enter_context(tc.psum_pool(name="psum", bufs=8))
+        psum = ctx.enter_context(tc.psum_pool(name="psum", bufs=1))
 
-        def bank(name):
-            return psum.tile([P, BANK], F32, tag="bank", name=name)
+        def bank(i, name):
+            return psum.tile([P, BANK], F32, tag=f"bank{i}", name=name)
 
-        gate_rows = keep.tile([P, P], F32)
+        gate_rows = keep.tile([P, P], F32, tag="picked")
         nc.gpsimd.memset(gate_rows[:], 0.0)
         head_plane = keep.tile([P, PASSES, HEAD], U8, align_bytes=64)
         nc.gpsimd.memset(head_plane[:].bitcast(I32), 0)
@@ -64,7 +64,7 @@ def tile_picked_wema_tanh_l_kernel(tc, x_words, x_scales, mem, w1, old, new, slo
             pattern=[[-1, P]],
             channel_multiplier=1,
         )
-        tail_plane = keep.tile([P, PASSES, T - HEAD], U8, tag="tail_plane", align_bytes=64)
+        tail_plane = keep.tile([P, PASSES, TAIL], U8, tag="tail_plane", align_bytes=64)
         nc.gpsimd.memset(tail_plane[:].bitcast(I32), 0)
 
         w_rows = w1.rearrange("(g p j) m -> g p j m", g=PASSES, j=4)
@@ -86,16 +86,21 @@ def tile_picked_wema_tanh_l_kernel(tc, x_words, x_scales, mem, w1, old, new, slo
 
         for q in range(QUADRANTS):
             load_scales(nc.sync, head_plane, q, 0, HEAD)
-        x = keep.tile([P, 2, PASSES, HEAD], U32, tag="x", align_bytes=64)
+        x = keep.tile([P, PASSES * T], U32, tag="x", align_bytes=64)
         x_rows = x_words.rearrange("g p n t -> p g (n t)").bitcast(I32)
-        for g in range(PASSES):
-            nc.sync.dma_start(out=x[:, 0, g, :].bitcast(I32), in_=x_rows[:, g, 0:HEAD])
-        nc.sync.dma_start(out=x[:, 1].bitcast(I32), in_=x_rows[:, :, HEAD:T])
+        for c0, n in spans(X_LOADS):
+            dst = x[:, PASSES * c0 : PASSES * (c0 + n)].bitcast(I32).rearrange("p (g n) -> p g n", g=PASSES)
+            nc.sync.dma_start(out=dst, in_=x_rows[:, :, c0 : c0 + n])
         for q, engine in enumerate((nc.gpsimd, nc.gpsimd, nc.sync, nc.sync)):
-            load_scales(engine, tail_plane, q, HEAD, T - HEAD)
+            load_scales(engine, tail_plane, q, HEAD, TAIL)
 
         def x_codes(g, c0, n):
-            return x[:, c0 // HEAD, g, c0 % HEAD : c0 % HEAD + n].bitcast(FP8X4)
+            start, width = [s for s in spans(X_LOADS) if s[0] <= c0][-1]
+            first = PASSES * start + g * width + c0 - start
+            return x[:, first : first + n].bitcast(FP8X4)
+
+        def entries(c0, n):
+            return window[:].indirect(offs[:, c0 // 16 : (c0 + n) // 16])
 
         w_grouped = keep.tile([P, PASSES, N, 4], BF16, align_bytes=64)
         for g in range(PASSES):
@@ -108,7 +113,7 @@ def tile_picked_wema_tanh_l_kernel(tc, x_words, x_scales, mem, w1, old, new, slo
             in_=w_grouped[:].rearrange("p g m j -> p (g m j)"),
         )
 
-        gate_turned = bank("gate_turned")
+        gate_turned = bank(0, "gate_turned")
         nc.tensor.transpose(gate_turned[:, 0:P], gate_rows[:], ident[:])
         gate_cols = keep.tile([P, 2, BLOCKS], F32)
         nc.scalar.copy(out=gate_cols[:], in_=gate_turned[:, 0 : 2 * BLOCKS].rearrange("p (v b) -> p v b", v=2))
@@ -118,28 +123,26 @@ def tile_picked_wema_tanh_l_kernel(tc, x_words, x_scales, mem, w1, old, new, slo
                 col = gate_cols[:, v, c0 // P + b : c0 // P + b + 1]
                 nc.tensor.transpose(dst[:, b * P : (b + 1) * P], col.to_broadcast([P, P]), ident[:])
 
-        old_all = keep.tile([P, T], F32)
-        for copy, (c0, n) in zip((nc.scalar.copy, nc.vector.tensor_copy, nc.scalar.copy), spans(OLD_COPIES)):
-            old_spread = bank(f"old_spread{c0}")
+        kept = keep.tile([P, T + 256], F32)
+        old_fused = kept[:, T - 256 : T + 256]
+        for i, (c0, n) in enumerate(spans((256, 256))):
+            old_spread = bank(1 + i, f"old_spread{c0}")
             spread(old_spread, 0, c0, n)
-            copy(out=old_all[:, c0 : c0 + n], in_=old_spread[:, 0:n])
-        new_spread = bank("new_spread")
-        spread(new_spread, 1, 0, HEAD)
+            nc.vector.tensor_copy(out=old_fused[:, c0 : c0 + n], in_=old_spread[:, 0:n])
+        new_head = bank(3, "new_head")
+        spread(new_head, 1, 0, HEAD)
+        old_tail = bank(4, "old_tail")
+        spread(old_tail, 0, HEAD, TAIL)
 
-        kept = keep.tile([P, T], F32)
-        for c0, n in spans(GATHERS):
-            nc.vector.tensor_tensor(
-                out=kept[:, c0 : c0 + n],
-                in0=window[:].indirect(offs[:, c0 // 16 : (c0 + n) // 16]),
-                in1=old_all[:, c0 : c0 + n],
-                op=ALU.mult,
-            )
+        for c0, n in spans((256, 256)):
+            nc.vector.tensor_tensor(out=kept[:, c0 : c0 + n], in0=entries(c0, n), in1=old_fused[:, c0 : c0 + n], op=ALU.mult)
+        picked = keep.tile([P, T - FUSED], F32, tag="picked")
+        nc.scalar.activation(out=picked[:], in_=entries(FUSED, T - FUSED), func=ACT.Copy)
 
-        fresh = keep.tile([P, T], F32)
         y_head = keep.tile([P, HEAD], F32)
-        accs = [bank(f"acc{c0}") for c0, n in spans(HEAD_GROUPS)]
-        for g in range(PASSES):
-            for acc, (c0, n) in zip(accs, spans(HEAD_GROUPS)):
+        for i, (c0, n) in enumerate(spans(HEAD_GROUPS)):
+            acc = bank(i, f"acc{c0}")
+            for g in range(PASSES):
                 nc.tensor.matmul_mx(
                     out=acc[:, 0:n],
                     lhsT=w_words[:, g * N : (g + 1) * N].bitcast(FP8X4),
@@ -149,17 +152,13 @@ def tile_picked_wema_tanh_l_kernel(tc, x_words, x_scales, mem, w1, old, new, slo
                     start=(g == 0),
                     stop=(g == PASSES - 1),
                 )
-        for acc, (c0, n) in zip(accs, spans(HEAD_GROUPS)):
             nc.scalar.activation(out=y_head[:, c0 : c0 + n], in_=acc[:, 0:n], func=ACT.Tanh, bias=zero_bias[:])
-        for c0, n in spans(HEAD_PRODUCTS):
-            nc.vector.tensor_tensor(
-                out=fresh[:, c0 : c0 + n], in0=y_head[:, c0 : c0 + n], in1=new_spread[:, c0 : c0 + n], op=ALU.mult
-            )
 
-        y_tail = keep.tile([P, T - HEAD], F32)
-        weighed = keep.tile([P, T - HEAD], F32)
-        for t0, n in spans(TAIL_GROUPS):
-            acc = bank(f"acc{HEAD + t0}")
+        fresh_tail = keep.tile([P, TAIL], F32)
+        y_tail = keep.tile([P, TAIL], F32)
+        weighed = keep.tile([P, TAIL], F32)
+        for i, (t0, n) in enumerate(spans(TAIL_GROUPS)):
+            acc = bank(5 + i, f"acc{HEAD + t0}")
             for b in range(n // P):
                 for g in range(PASSES):
                     nc.tensor.matmul_mx(
@@ -173,8 +172,8 @@ def tile_picked_wema_tanh_l_kernel(tc, x_words, x_scales, mem, w1, old, new, slo
                     )
             nc.scalar.activation(out=y_tail[:, t0 : t0 + n], in_=acc[:, 0:n], func=ACT.Tanh, bias=zero_bias[:])
         turned = []
-        for t0, n in spans(TAIL_GROUPS):
-            back = bank(f"back{t0}")
+        for i, (t0, n) in enumerate(spans(TAIL_GROUPS)):
+            back = bank(i, f"back{t0}")
             for b in range(n // P):
                 cols = slice(t0 + b * P, t0 + (b + 1) * P)
                 block = (HEAD + t0) // P + b
@@ -184,14 +183,26 @@ def tile_picked_wema_tanh_l_kernel(tc, x_words, x_scales, mem, w1, old, new, slo
                 nc.tensor.transpose(back[:, b * P : (b + 1) * P], weighed[:, cols], ident[:])
             turned.append(back)
         for back, (t0, n) in zip(turned, spans(TAIL_GROUPS)):
-            nc.scalar.copy(out=fresh[:, HEAD + t0 : HEAD + t0 + n], in_=back[:, 0:n])
+            nc.scalar.copy(out=fresh_tail[:, t0 : t0 + n], in_=back[:, 0:n])
 
-        for c0, n in spans(SCATTERS):
-            nc.vector.tensor_tensor(
-                out=window[:].indirect(offs[:, c0 // 16 : (c0 + n) // 16]),
-                in0=kept[:, c0 : c0 + n],
-                in1=fresh[:, c0 : c0 + n],
-                op=ALU.add,
-            )
+        def product(dst, a, b):
+            nc.vector.tensor_tensor(out=dst, in0=a, in1=b, op=ALU.mult)
+
+        def scatter(c0, n, a, b):
+            nc.vector.tensor_tensor(out=entries(c0, n), in0=a, in1=b, op=ALU.add)
+
+        def weigh_picked(c0, n):
+            product(kept[:, c0 : c0 + n], picked[:, c0 - FUSED : c0 - FUSED + n], old_tail[:, c0 - HEAD : c0 - HEAD + n])
+
+        first_fresh = kept[:, FUSED : FUSED + FIRST]
+        fresh = keep.tile([P, HEAD - FIRST], F32)
+        weigh_picked(FUSED + LATE, T - FUSED - LATE)
+        product(first_fresh, y_head[:, 0:FIRST], new_head[:, 0:FIRST])
+        product(fresh[:, 0:P], y_head[:, FIRST : FIRST + P], new_head[:, FIRST : FIRST + P])
+        scatter(0, FIRST, kept[:, 0:FIRST], first_fresh)
+        product(fresh[:, P:], y_head[:, FIRST + P :], new_head[:, FIRST + P :])
+        weigh_picked(FUSED, LATE)
+        scatter(FIRST, HEAD - FIRST, kept[:, FIRST:HEAD], fresh[:])
+        scatter(HEAD, TAIL, kept[:, HEAD:T], fresh_tail[:])
 
         nc.sync.dma_start(out=out, in_=window[:])

@@ -80,8 +80,8 @@ def tile_picked_wema_tanh_l_kernel(tc, x_words, x_scales, mem, w1, old, new, slo
 
         def load_scales(engine, plane, q, c0, n):
             engine.dma_start(
-                out=plane[32 * q : 32 * q + 4].bitcast(I32),
-                in_=x_scales[:, 4 * q : 4 * q + 4, c0 : c0 + n].bitcast(I32).rearrange("g r n -> r g n"),
+                out=plane[q:P:32].bitcast(I32),
+                in_=x_scales[:, q:16:4, c0 : c0 + n].bitcast(I32).rearrange("g q n -> q g n"),
             )
 
         for q in range(QUADRANTS):

@@ -44,10 +44,10 @@ def tile_picked_wema_tanh_l_kernel(tc, x_words, x_scales, mem, w1, old, new, slo
         def bank(i, name):
             return psum.tile([P, BANK], F32, tag=f"bank{i}", name=name)
 
-        gate_rows = keep.tile([P, P], F32, tag="picked")
-        nc.gpsimd.memset(gate_rows[:], 0.0)
         head_plane = keep.tile([P, PASSES, HEAD], U8, align_bytes=64)
         nc.gpsimd.memset(head_plane[:].bitcast(I32), 0)
+        gate_rows = keep.tile([P, P], F32, tag="picked")
+        nc.gpsimd.memset(gate_rows[0 : P - 2 * BLOCKS, :], 0.0)
         zero_in = keep.tile([P, 1], F32, tag="x", align_bytes=64)
         nc.vector.memset(zero_in[:], 0.0)
         zero_bias = keep.tile([P, 1], F32)
@@ -67,16 +67,12 @@ def tile_picked_wema_tanh_l_kernel(tc, x_words, x_scales, mem, w1, old, new, slo
         tail_plane = keep.tile([P, PASSES, TAIL], U8, tag="tail_plane", align_bytes=64)
         nc.gpsimd.memset(tail_plane[:].bitcast(I32), 0)
 
-        w_rows = w1.rearrange("(g p j) m -> g p j m", g=PASSES, j=4)
-        w_raw = [keep.tile([P, 4, N], F32, name=f"w_raw{g}") for g in range(PASSES)]
-        nc.sync.dma_start(out=w_raw[0][:], in_=w_rows[0])
+        w_raw = keep.tile([P, PASSES, 4, N], F32)
+        nc.sync.dma_start(out=w_raw[:], in_=w1.rearrange("(g p j) m -> p g j m", g=PASSES, j=4))
         offs = keep.tile([P, T // 16], U16)
         nc.sync.dma_start(out=offs[:], in_=slot)
-        nc.sync.dma_start(out=gate_rows[0:BLOCKS, :], in_=old[0, :].rearrange("(b c) -> b c", c=P))
-        nc.sync.dma_start(out=gate_rows[BLOCKS : 2 * BLOCKS, :], in_=new[0, :].rearrange("(b c) -> b c", c=P))
-        nc.sync.dma_start(out=w_raw[1][:], in_=w_rows[1])
-        window = keep.tile([P, U], F32)
-        nc.sync.dma_start(out=window[:], in_=mem)
+        nc.sync.dma_start(out=gate_rows[P - 2 * BLOCKS : P - BLOCKS, :], in_=old[0, :].rearrange("(b c) -> b c", c=P))
+        nc.sync.dma_start(out=gate_rows[P - BLOCKS : P, :], in_=new[0, :].rearrange("(b c) -> b c", c=P))
 
         def load_scales(engine, plane, q, c0, n):
             engine.dma_start(
@@ -84,13 +80,20 @@ def tile_picked_wema_tanh_l_kernel(tc, x_words, x_scales, mem, w1, old, new, slo
                 in_=x_scales[:, q:16:4, c0 : c0 + n].bitcast(I32).rearrange("g q n -> q g n"),
             )
 
-        for q in range(QUADRANTS):
+        load_scales(nc.sync, head_plane, 0, 0, HEAD)
+        window = keep.tile([P, U], F32)
+        nc.sync.dma_start(out=window[:], in_=mem)
+        for q in range(1, QUADRANTS):
             load_scales(nc.sync, head_plane, q, 0, HEAD)
         x = keep.tile([P, PASSES * T], U32, tag="x", align_bytes=64)
         x_rows = x_words.rearrange("g p n t -> p g (n t)").bitcast(I32)
         for c0, n in spans(X_LOADS):
             dst = x[:, PASSES * c0 : PASSES * (c0 + n)].bitcast(I32).rearrange("p (g n) -> p g n", g=PASSES)
-            nc.sync.dma_start(out=dst, in_=x_rows[:, :, c0 : c0 + n])
+            if c0 == 0:
+                for g in range(PASSES):
+                    nc.sync.dma_start(out=dst[:, g], in_=x_rows[:, g, c0 : c0 + n])
+            else:
+                nc.sync.dma_start(out=dst, in_=x_rows[:, :, c0 : c0 + n])
         for q, engine in enumerate((nc.gpsimd, nc.gpsimd, nc.sync, nc.sync)):
             load_scales(engine, tail_plane, q, HEAD, TAIL)
 
@@ -104,7 +107,7 @@ def tile_picked_wema_tanh_l_kernel(tc, x_words, x_scales, mem, w1, old, new, slo
 
         w_grouped = keep.tile([P, PASSES, N, 4], BF16, align_bytes=64)
         for g in range(PASSES):
-            nc.vector.tensor_copy(out=w_grouped[:, g], in_=w_raw[g][:].rearrange("p j m -> p m j"))
+            nc.vector.tensor_copy(out=w_grouped[:, g], in_=w_raw[:, g].rearrange("p j m -> p m j"))
         w_words = keep.tile([P, PASSES * N], U32, align_bytes=64)
         w_plane = keep.tile([P, PASSES * N], U8, align_bytes=64)
         nc.vector.quantize_mx(
@@ -116,7 +119,7 @@ def tile_picked_wema_tanh_l_kernel(tc, x_words, x_scales, mem, w1, old, new, slo
         gate_turned = bank(0, "gate_turned")
         nc.tensor.transpose(gate_turned[:, 0:P], gate_rows[:], ident[:])
         gate_cols = keep.tile([P, 2, BLOCKS], F32)
-        nc.scalar.copy(out=gate_cols[:], in_=gate_turned[:, 0 : 2 * BLOCKS].rearrange("p (v b) -> p v b", v=2))
+        nc.scalar.copy(out=gate_cols[:], in_=gate_turned[:, P - 2 * BLOCKS : P].rearrange("p (v b) -> p v b", v=2))
 
         def spread(dst, v, c0, n):
             for b in range(n // P):
@@ -140,18 +143,22 @@ def tile_picked_wema_tanh_l_kernel(tc, x_words, x_scales, mem, w1, old, new, slo
         nc.scalar.activation(out=picked[:], in_=entries(FUSED, T - FUSED), func=ACT.Copy)
 
         y_head = keep.tile([P, HEAD], F32)
-        for i, (c0, n) in enumerate(spans(HEAD_GROUPS)):
-            acc = bank(i, f"acc{c0}")
+        groups = spans(HEAD_GROUPS)
+        accs = [bank(i, f"acc{c0}") for i, (c0, n) in enumerate(groups)]
+        for together in ((0, 1), (2,)):
             for g in range(PASSES):
-                nc.tensor.matmul_mx(
-                    out=acc[:, 0:n],
-                    lhsT=w_words[:, g * N : (g + 1) * N].bitcast(FP8X4),
-                    lhsT_scale=w_plane[:, g * N : (g + 1) * N],
-                    rhs=x_codes(g, c0, n),
-                    rhs_scale=head_plane[:, g, c0 : c0 + n],
-                    start=(g == 0),
-                    stop=(g == PASSES - 1),
-                )
+                for i in together:
+                    c0, n = groups[i]
+                    nc.tensor.matmul_mx(
+                        out=accs[i][:, 0:n],
+                        lhsT=w_words[:, g * N : (g + 1) * N].bitcast(FP8X4),
+                        lhsT_scale=w_plane[:, g * N : (g + 1) * N],
+                        rhs=x_codes(g, c0, n),
+                        rhs_scale=head_plane[:, g, c0 : c0 + n],
+                        start=(g == 0),
+                        stop=(g == PASSES - 1),
+                    )
+        for acc, (c0, n) in zip(accs, groups):
             nc.scalar.activation(out=y_head[:, c0 : c0 + n], in_=acc[:, 0:n], func=ACT.Tanh, bias=zero_bias[:])
 
         fresh_tail = keep.tile([P, TAIL], F32)

@@ -26,6 +26,7 @@ TAIL = T - HEAD
 FUSED = HEAD
 FIRST = P
 LATE = 256
+EARLY = HEAD + P
 X_LOADS = (256, 256, 512)
 HEAD_GROUPS = (128, 128, 256)
 TAIL_GROUPS = (128, 256, 128)
@@ -44,7 +45,7 @@ def tile_picked_wema_tanh_l_kernel(tc, x_words, x_scales, mem, w1, old, new, slo
         def bank(i, name):
             return psum.tile([P, BANK], F32, tag=f"bank{i}", name=name)
 
-        head_plane = keep.tile([P, PASSES, HEAD], U8, align_bytes=64)
+        head_plane = keep.tile([P, PASSES, EARLY], U8, align_bytes=64)
         nc.gpsimd.memset(head_plane[:].bitcast(I32), 0)
         gate_rows = keep.tile([P, P], F32, tag="picked")
         nc.gpsimd.memset(gate_rows[0 : P - 2 * BLOCKS, :], 0.0)
@@ -64,7 +65,7 @@ def tile_picked_wema_tanh_l_kernel(tc, x_words, x_scales, mem, w1, old, new, slo
             pattern=[[-1, P]],
             channel_multiplier=1,
         )
-        tail_plane = keep.tile([P, PASSES, TAIL], U8, tag="tail_plane", align_bytes=64)
+        tail_plane = keep.tile([P, PASSES, T - EARLY], U8, tag="tail_plane", align_bytes=64)
         nc.gpsimd.memset(tail_plane[:].bitcast(I32), 0)
 
         w_raw = keep.tile([P, PASSES, 4, N], F32)
@@ -80,11 +81,11 @@ def tile_picked_wema_tanh_l_kernel(tc, x_words, x_scales, mem, w1, old, new, slo
                 in_=x_scales[:, q:16:4, c0 : c0 + n].bitcast(I32).rearrange("g q n -> q g n"),
             )
 
-        load_scales(nc.sync, head_plane, 0, 0, HEAD)
+        load_scales(nc.sync, head_plane, 0, 0, EARLY)
         window = keep.tile([P, U], F32)
         nc.sync.dma_start(out=window[:], in_=mem)
         for q in range(1, QUADRANTS):
-            load_scales(nc.sync, head_plane, q, 0, HEAD)
+            load_scales(nc.sync, head_plane, q, 0, EARLY)
         x = keep.tile([P, PASSES * T], U32, tag="x", align_bytes=64)
         x_rows = x_words.rearrange("g p n t -> p g (n t)").bitcast(I32)
         for c0, n in spans(X_LOADS):
@@ -95,12 +96,15 @@ def tile_picked_wema_tanh_l_kernel(tc, x_words, x_scales, mem, w1, old, new, slo
             else:
                 nc.sync.dma_start(out=dst, in_=x_rows[:, :, c0 : c0 + n])
         for q, engine in enumerate((nc.gpsimd, nc.gpsimd, nc.sync, nc.sync)):
-            load_scales(engine, tail_plane, q, HEAD, TAIL)
+            load_scales(engine, tail_plane, q, EARLY, T - EARLY)
 
         def x_codes(g, c0, n):
             start, width = [s for s in spans(X_LOADS) if s[0] <= c0][-1]
             first = PASSES * start + g * width + c0 - start
             return x[:, first : first + n].bitcast(FP8X4)
+
+        def x_scale(g, c0, n):
+            return head_plane[:, g, c0 : c0 + n] if c0 < EARLY else tail_plane[:, g, c0 - EARLY : c0 - EARLY + n]
 
         def entries(c0, n):
             return window[:].indirect(offs[:, c0 // 16 : (c0 + n) // 16])
@@ -154,7 +158,7 @@ def tile_picked_wema_tanh_l_kernel(tc, x_words, x_scales, mem, w1, old, new, slo
                         lhsT=w_words[:, g * N : (g + 1) * N].bitcast(FP8X4),
                         lhsT_scale=w_plane[:, g * N : (g + 1) * N],
                         rhs=x_codes(g, c0, n),
-                        rhs_scale=head_plane[:, g, c0 : c0 + n],
+                        rhs_scale=x_scale(g, c0, n),
                         start=(g == 0),
                         stop=(g == PASSES - 1),
                     )
@@ -164,6 +168,11 @@ def tile_picked_wema_tanh_l_kernel(tc, x_words, x_scales, mem, w1, old, new, slo
         fresh_tail = keep.tile([P, TAIL], F32)
         y_tail = keep.tile([P, TAIL], F32)
         weighed = keep.tile([P, TAIL], F32)
+
+        def weigh(t0, src):
+            block = (HEAD + t0) // P
+            nc.scalar.activation(out=weighed[:, t0 : t0 + P], in_=src, func=ACT.Copy, scale=gate_cols[:, 1, block : block + 1])
+
         for i, (t0, n) in enumerate(spans(TAIL_GROUPS)):
             acc = bank(5 + i, f"acc{HEAD + t0}")
             for b in range(n // P):
@@ -171,22 +180,23 @@ def tile_picked_wema_tanh_l_kernel(tc, x_words, x_scales, mem, w1, old, new, slo
                     nc.tensor.matmul_mx(
                         out=acc[:, b * P : (b + 1) * P],
                         lhsT=x_codes(g, HEAD + t0 + b * P, P),
-                        lhsT_scale=tail_plane[:, g, t0 + b * P : t0 + (b + 1) * P],
+                        lhsT_scale=x_scale(g, HEAD + t0 + b * P, P),
                         rhs=w_words[:, g * N : (g + 1) * N].bitcast(FP8X4),
                         rhs_scale=w_plane[:, g * N : (g + 1) * N],
                         start=(g == 0),
                         stop=(g == PASSES - 1),
                     )
-            nc.scalar.activation(out=y_tail[:, t0 : t0 + n], in_=acc[:, 0:n], func=ACT.Tanh, bias=zero_bias[:])
+            y0 = max(t0, P)
+            nc.scalar.activation(out=y_tail[:, y0 : y0 + n], in_=acc[:, 0:n], func=ACT.Tanh, bias=zero_bias[:])
+            if i == 0:
+                weigh(0, y_tail[:, P : 2 * P])
         turned = []
         for i, (t0, n) in enumerate(spans(TAIL_GROUPS)):
             back = bank(i, f"back{t0}")
             for b in range(n // P):
                 cols = slice(t0 + b * P, t0 + (b + 1) * P)
-                block = (HEAD + t0) // P + b
-                nc.scalar.activation(
-                    out=weighed[:, cols], in_=y_tail[:, cols], func=ACT.Copy, scale=gate_cols[:, 1, block : block + 1]
-                )
+                if i > 0:
+                    weigh(cols.start, y_tail[:, cols])
                 nc.tensor.transpose(back[:, b * P : (b + 1) * P], weighed[:, cols], ident[:])
             turned.append(back)
         for back, (t0, n) in zip(turned, spans(TAIL_GROUPS)):

@@ -23,7 +23,7 @@ QUADRANTS = 4
 BLOCKS = T // P
 HEAD = BANK
 TAIL = T - HEAD
-FUSED = HEAD
+FUSED = 576
 FIRST = P
 LATE = 256
 EARLY = HEAD + P
@@ -130,18 +130,18 @@ def tile_picked_wema_tanh_l_kernel(tc, x_words, x_scales, mem, w1, old, new, slo
                 col = gate_cols[:, v, c0 // P + b : c0 // P + b + 1]
                 nc.tensor.transpose(dst[:, b * P : (b + 1) * P], col.to_broadcast([P, P]), ident[:])
 
-        kept = keep.tile([P, T + 256], F32)
-        old_fused = kept[:, T - 256 : T + 256]
-        for i, (c0, n) in enumerate(spans((256, 256))):
+        kept = keep.tile([P, 2 * FUSED + LATE], F32)
+        old_fused = kept[:, FUSED + LATE :]
+        for i, (c0, n) in enumerate(spans((256, FUSED - 256))):
             old_spread = bank(1 + i, f"old_spread{c0}")
-            spread(old_spread, 0, c0, n)
+            spread(old_spread, 0, c0, n + -n % P)
             nc.vector.tensor_copy(out=old_fused[:, c0 : c0 + n], in_=old_spread[:, 0:n])
         new_head = bank(3, "new_head")
         spread(new_head, 1, 0, HEAD)
         old_tail = bank(4, "old_tail")
         spread(old_tail, 0, HEAD, TAIL)
 
-        for c0, n in spans((256, 256)):
+        for c0, n in spans((256, FUSED - 256)):
             nc.vector.tensor_tensor(out=kept[:, c0 : c0 + n], in0=entries(c0, n), in1=old_fused[:, c0 : c0 + n], op=ALU.mult)
         picked = keep.tile([P, T - FUSED], F32, tag="picked")
         nc.scalar.activation(out=picked[:], in_=entries(FUSED, T - FUSED), func=ACT.Copy)

@@ -25,11 +25,11 @@ HEAD = BANK
 TAIL = T - HEAD
 FUSED = 576
 FIRST = P
-LATE = 256
-EARLY = HEAD + P
+LATE = 192
+EARLY = HEAD
 X_LOADS = (256, 256, 512)
 HEAD_GROUPS = (128, 128, 256)
-TAIL_GROUPS = (128, 256, 128)
+BACK_GROUPS = (384, 128)
 
 
 def spans(widths, start=0):
@@ -72,8 +72,8 @@ def tile_picked_wema_tanh_l_kernel(tc, x_words, x_scales, mem, w1, old, new, slo
         nc.sync.dma_start(out=w_raw[:], in_=w1.rearrange("(g p j) m -> p g j m", g=PASSES, j=4))
         offs = keep.tile([P, T // 16], U16)
         nc.sync.dma_start(out=offs[:], in_=slot)
-        nc.sync.dma_start(out=gate_rows[P - 2 * BLOCKS : P - BLOCKS, :], in_=old[0, :].rearrange("(b c) -> b c", c=P))
-        nc.sync.dma_start(out=gate_rows[P - BLOCKS : P, :], in_=new[0, :].rearrange("(b c) -> b c", c=P))
+        nc.scalar.dma_start(out=gate_rows[P - 2 * BLOCKS : P - BLOCKS, :], in_=old[0, :].rearrange("(b c) -> b c", c=P))
+        nc.scalar.dma_start(out=gate_rows[P - BLOCKS : P, :], in_=new[0, :].rearrange("(b c) -> b c", c=P))
 
         def load_scales(engine, plane, q, c0, n):
             engine.dma_start(
@@ -169,37 +169,26 @@ def tile_picked_wema_tanh_l_kernel(tc, x_words, x_scales, mem, w1, old, new, slo
         y_tail = keep.tile([P, TAIL], F32)
         weighed = keep.tile([P, TAIL], F32)
 
-        def weigh(t0, src):
+        for t0 in range(0, TAIL, P):
+            acc = bank((5 + t0 // P) % 8, f"acc{HEAD + t0}")
+            for g in range(PASSES):
+                nc.tensor.matmul_mx(
+                    out=acc[:, 0:P],
+                    lhsT=x_codes(g, HEAD + t0, P),
+                    lhsT_scale=x_scale(g, HEAD + t0, P),
+                    rhs=w_words[:, g * N : (g + 1) * N].bitcast(FP8X4),
+                    rhs_scale=w_plane[:, g * N : (g + 1) * N],
+                    start=(g == 0),
+                    stop=(g == PASSES - 1),
+                )
+            nc.scalar.activation(out=y_tail[:, t0 : t0 + P], in_=acc[:, 0:P], func=ACT.Tanh, bias=zero_bias[:])
+        for t0 in range(0, TAIL, P):
             block = (HEAD + t0) // P
-            nc.scalar.activation(out=weighed[:, t0 : t0 + P], in_=src, func=ACT.Copy, scale=gate_cols[:, 1, block : block + 1])
-
-        for i, (t0, n) in enumerate(spans(TAIL_GROUPS)):
-            acc = bank(5 + i, f"acc{HEAD + t0}")
+            nc.scalar.activation(out=weighed[:, t0 : t0 + P], in_=y_tail[:, t0 : t0 + P], func=ACT.Copy, scale=gate_cols[:, 1, block : block + 1])
+        for i, (t0, n) in enumerate(spans(BACK_GROUPS)):
+            back = bank(1 + i, f"back{t0}")
             for b in range(n // P):
-                for g in range(PASSES):
-                    nc.tensor.matmul_mx(
-                        out=acc[:, b * P : (b + 1) * P],
-                        lhsT=x_codes(g, HEAD + t0 + b * P, P),
-                        lhsT_scale=x_scale(g, HEAD + t0 + b * P, P),
-                        rhs=w_words[:, g * N : (g + 1) * N].bitcast(FP8X4),
-                        rhs_scale=w_plane[:, g * N : (g + 1) * N],
-                        start=(g == 0),
-                        stop=(g == PASSES - 1),
-                    )
-            y0 = max(t0, P)
-            nc.scalar.activation(out=y_tail[:, y0 : y0 + n], in_=acc[:, 0:n], func=ACT.Tanh, bias=zero_bias[:])
-            if i == 0:
-                weigh(0, y_tail[:, P : 2 * P])
-        turned = []
-        for i, (t0, n) in enumerate(spans(TAIL_GROUPS)):
-            back = bank(i, f"back{t0}")
-            for b in range(n // P):
-                cols = slice(t0 + b * P, t0 + (b + 1) * P)
-                if i > 0:
-                    weigh(cols.start, y_tail[:, cols])
-                nc.tensor.transpose(back[:, b * P : (b + 1) * P], weighed[:, cols], ident[:])
-            turned.append(back)
-        for back, (t0, n) in zip(turned, spans(TAIL_GROUPS)):
+                nc.tensor.transpose(back[:, b * P : (b + 1) * P], weighed[:, t0 + b * P : t0 + (b + 1) * P], ident[:])
             nc.scalar.copy(out=fresh_tail[:, t0 : t0 + n], in_=back[:, 0:n])
 
         def product(dst, a, b):

from contextlib import ExitStack

import concourse.mybir as mybir

K, T, N, U = 1024, 1024, 128, 2048
FLOPS = 2 * K * T * N
BYTES = K * T + K * T // 32 + 4 * (K * N + 2 * N * U + 2 * T) + 2 * 128 * (T // 16)

F32 = mybir.dt.float32
BF16 = mybir.dt.bfloat16
I32 = mybir.dt.int32
U32 = mybir.dt.uint32
U16 = mybir.dt.uint16
U8 = mybir.dt.uint8
FP8X4 = mybir.dt.float8_e4m3fn_x4
ACT = mybir.ActivationFunctionType
ALU = mybir.AluOpType

P = 128
BANK = 512
PASSES = K // 512
QUADRANTS = 4
BLOCKS = T // P
HEAD = BANK
TAIL = T - HEAD
FUSED = 576
FIRST = P
LATE = 192
EARLY = HEAD
X_LOADS = (256, 256, 512)
HEAD_GROUPS = (128, 128, 256)
BACK_GROUPS = (384, 128)


def spans(widths, start=0):
    return [(start + sum(widths[:i]), w) for i, w in enumerate(widths)]


def tile_picked_wema_tanh_l_kernel(tc, x_words, x_scales, mem, w1, old, new, slot, out):
    nc = tc.nc
    with ExitStack() as ctx:
        keep = ctx.enter_context(tc.tile_pool(name="keep", bufs=1))
        psum = ctx.enter_context(tc.psum_pool(name="psum", bufs=1))

        def bank(i, name):
            return psum.tile([P, BANK], F32, tag=f"bank{i}", name=name)

        head_plane = keep.tile([P, PASSES, EARLY], U8, align_bytes=64)
        nc.gpsimd.memset(head_plane[:].bitcast(I32), 0)
        gate_rows = keep.tile([P, P], F32, tag="picked")
        nc.gpsimd.memset(gate_rows[0 : P - 2 * BLOCKS, :], 0.0)
        zero_in = keep.tile([P, 1], F32, tag="x", align_bytes=64)
        nc.vector.memset(zero_in[:], 0.0)
        zero_bias = keep.tile([P, 1], F32)
        nc.scalar.activation(out=zero_bias[:], in_=zero_in[:], func=ACT.Tanh)
        ident = keep.tile([P, P], F32)
        ident_zeros = keep.tile([P, P], F32, tag="tail_plane", align_bytes=64)
        nc.gpsimd.memset(ident_zeros[:], 0.0)
        nc.gpsimd.affine_select(
            out=ident[:],
            in_=ident_zeros[:],
            compare_op=ALU.not_equal,
            fill=1.0,
            base=0,
            pattern=[[-1, P]],
            channel_multiplier=1,
        )
        tail_plane = keep.tile([P, PASSES, T - EARLY], U8, tag="tail_plane", align_bytes=64)
        nc.gpsimd.memset(tail_plane[:].bitcast(I32), 0)

        w_raw = keep.tile([P, PASSES, 4, N], F32)
        nc.sync.dma_start(out=w_raw[:], in_=w1.rearrange("(g p j) m -> p g j m", g=PASSES, j=4))
        offs = keep.tile([P, T // 16], U16)
        nc.sync.dma_start(out=offs[:], in_=slot)
        nc.scalar.dma_start(out=gate_rows[P - 2 * BLOCKS : P - BLOCKS, :], in_=old[0, :].rearrange("(b c) -> b c", c=P))
        nc.scalar.dma_start(out=gate_rows[P - BLOCKS : P, :], in_=new[0, :].rearrange("(b c) -> b c", c=P))

        def load_scales(engine, plane, q, c0, n):
            engine.dma_start(
                out=plane[q:P:32].bitcast(I32),
                in_=x_scales[:, q:16:4, c0 : c0 + n].bitcast(I32).rearrange("g q n -> q g n"),
            )

        load_scales(nc.sync, head_plane, 0, 0, EARLY)
        window = keep.tile([P, U], F32)
        nc.sync.dma_start(out=window[:], in_=mem)
        for q in range(1, QUADRANTS):
            load_scales(nc.sync, head_plane, q, 0, EARLY)
        x = keep.tile([P, PASSES * T], U32, tag="x", align_bytes=64)
        x_rows = x_words.rearrange("g p n t -> p g (n t)").bitcast(I32)
        for c0, n in spans(X_LOADS):
            dst = x[:, PASSES * c0 : PASSES * (c0 + n)].bitcast(I32).rearrange("p (g n) -> p g n", g=PASSES)
            if c0 == 0:
                for g in range(PASSES):
                    nc.sync.dma_start(out=dst[:, g], in_=x_rows[:, g, c0 : c0 + n])
            else:
                nc.sync.dma_start(out=dst, in_=x_rows[:, :, c0 : c0 + n])
        for q, engine in enumerate((nc.gpsimd, nc.gpsimd, nc.sync, nc.sync)):
            load_scales(engine, tail_plane, q, EARLY, T - EARLY)

        def x_codes(g, c0, n):
            start, width = [s for s in spans(X_LOADS) if s[0] <= c0][-1]
            first = PASSES * start + g * width + c0 - start
            return x[:, first : first + n].bitcast(FP8X4)

        def x_scale(g, c0, n):
            return head_plane[:, g, c0 : c0 + n] if c0 < EARLY else tail_plane[:, g, c0 - EARLY : c0 - EARLY + n]

        def entries(c0, n):
            return window[:].indirect(offs[:, c0 // 16 : (c0 + n) // 16])

        w_grouped = keep.tile([P, PASSES, N, 4], BF16, align_bytes=64)
        for g in range(PASSES):
            nc.vector.tensor_copy(out=w_grouped[:, g], in_=w_raw[:, g].rearrange("p j m -> p m j"))
        w_words = keep.tile([P, PASSES * N], U32, align_bytes=64)
        w_plane = keep.tile([P, PASSES * N], U8, align_bytes=64)
        nc.vector.quantize_mx(
            out=w_words[:].bitcast(FP8X4),
            scales=w_plane[:],
            in_=w_grouped[:].rearrange("p g m j -> p (g m j)"),
        )

        gate_turned = bank(0, "gate_turned")
        nc.tensor.transpose(gate_turned[:, 0:P], gate_rows[:], ident[:])
        gate_cols = keep.tile([P, 2, BLOCKS], F32)
        nc.scalar.copy(out=gate_cols[:], in_=gate_turned[:, P - 2 * BLOCKS : P].rearrange("p (v b) -> p v b", v=2))

        def spread(dst, v, c0, n):
            for b in range(n // P):
                col = gate_cols[:, v, c0 // P + b : c0 // P + b + 1]
                nc.tensor.transpose(dst[:, b * P : (b + 1) * P], col.to_broadcast([P, P]), ident[:])

        kept = keep.tile([P, 2 * FUSED + LATE], F32)
        old_fused = kept[:, FUSED + LATE :]
        for i, (c0, n) in enumerate(spans((256, FUSED - 256))):
            old_spread = bank(1 + i, f"old_spread{c0}")
            spread(old_spread, 0, c0, n + -n % P)
            nc.vector.tensor_copy(out=old_fused[:, c0 : c0 + n], in_=old_spread[:, 0:n])
        new_head = bank(3, "new_head")
        spread(new_head, 1, 0, HEAD)
        old_tail = bank(4, "old_tail")
        spread(old_tail, 0, HEAD, TAIL)

        for c0, n in spans((256, FUSED - 256)):
            nc.vector.tensor_tensor(out=kept[:, c0 : c0 + n], in0=entries(c0, n), in1=old_fused[:, c0 : c0 + n], op=ALU.mult)
        picked = keep.tile([P, T - FUSED], F32, tag="picked")
        nc.scalar.activation(out=picked[:], in_=entries(FUSED, T - FUSED), func=ACT.Copy)

        y_head = keep.tile([P, HEAD], F32)
        groups = spans(HEAD_GROUPS)
        accs = [bank(i, f"acc{c0}") for i, (c0, n) in enumerate(groups)]
        for together in ((0, 1), (2,)):
            for g in range(PASSES):
                for i in together:
                    c0, n = groups[i]
                    nc.tensor.matmul_mx(
                        out=accs[i][:, 0:n],
                        lhsT=w_words[:, g * N : (g + 1) * N].bitcast(FP8X4),
                        lhsT_scale=w_plane[:, g * N : (g + 1) * N],
                        rhs=x_codes(g, c0, n),
                        rhs_scale=x_scale(g, c0, n),
                        start=(g == 0),
                        stop=(g == PASSES - 1),
                    )
        for acc, (c0, n) in zip(accs, groups):
            nc.scalar.activation(out=y_head[:, c0 : c0 + n], in_=acc[:, 0:n], func=ACT.Tanh, bias=zero_bias[:])

        fresh_tail = keep.tile([P, TAIL], F32)
        y_tail = keep.tile([P, TAIL], F32)
        weighed = keep.tile([P, TAIL], F32)

        for t0 in range(0, TAIL, P):
            acc = bank((5 + t0 // P) % 8, f"acc{HEAD + t0}")
            for g in range(PASSES):
                nc.tensor.matmul_mx(
                    out=acc[:, 0:P],
                    lhsT=x_codes(g, HEAD + t0, P),
                    lhsT_scale=x_scale(g, HEAD + t0, P),
                    rhs=w_words[:, g * N : (g + 1) * N].bitcast(FP8X4),
                    rhs_scale=w_plane[:, g * N : (g + 1) * N],
                    start=(g == 0),
                    stop=(g == PASSES - 1),
                )
            nc.scalar.activation(out=y_tail[:, t0 : t0 + P], in_=acc[:, 0:P], func=ACT.Tanh, bias=zero_bias[:])
        for t0 in range(0, TAIL, P):
            block = (HEAD + t0) // P
            nc.scalar.activation(out=weighed[:, t0 : t0 + P], in_=y_tail[:, t0 : t0 + P], func=ACT.Copy, scale=gate_cols[:, 1, block : block + 1])
        for i, (t0, n) in enumerate(spans(BACK_GROUPS)):
            back = bank(1 + i, f"back{t0}")
            for b in range(n // P):
                nc.tensor.transpose(back[:, b * P : (b + 1) * P], weighed[:, t0 + b * P : t0 + (b + 1) * P], ident[:])
            nc.scalar.copy(out=fresh_tail[:, t0 : t0 + n], in_=back[:, 0:n])

        def product(dst, a, b):
            nc.vector.tensor_tensor(out=dst, in0=a, in1=b, op=ALU.mult)

        def scatter(c0, n, a, b):
            nc.vector.tensor_tensor(out=entries(c0, n), in0=a, in1=b, op=ALU.add)

        def weigh_picked(c0, n):
            product(kept[:, c0 : c0 + n], picked[:, c0 - FUSED : c0 - FUSED + n], old_tail[:, c0 - HEAD : c0 - HEAD + n])

        first_fresh = kept[:, FUSED : FUSED + FIRST]
        fresh = keep.tile([P, HEAD - FIRST], F32)
        weigh_picked(FUSED + LATE, T - FUSED - LATE)
        product(first_fresh, y_head[:, 0:FIRST], new_head[:, 0:FIRST])
        product(fresh[:, 0:P], y_head[:, FIRST : FIRST + P], new_head[:, FIRST : FIRST + P])
        scatter(0, FIRST, kept[:, 0:FIRST], first_fresh)
        product(fresh[:, P:], y_head[:, FIRST + P :], new_head[:, FIRST + P :])
        weigh_picked(FUSED, LATE)
        scatter(FIRST, HEAD - FIRST, kept[:, FIRST:HEAD], fresh[:])
        scatter(HEAD, TAIL, kept[:, HEAD:T], fresh_tail[:])

        nc.sync.dma_start(out=out, in_=window[:])
